import numpy as np, ml_dtypes
CORES = [5,29,101,125,133,157,229,253]
N = 8
import mx_ref
BF = ml_dtypes.bfloat16
def f(rng, *shape):
    return mx_ref.flush((rng.standard_normal(shape, dtype=np.float32) * np.exp2(rng.integers(-2, 3, shape[:-1] + (1,)))).astype(BF))
def wide(rng, *shape, cols=0):
    v = rng.standard_normal(shape, dtype=np.float32) * np.exp2(rng.integers(-12, 13, shape)).astype(np.float32)
    if cols: v *= np.repeat(np.exp2(rng.integers(-cols, cols + 1, shape[:-2] + (1, shape[-1] // 4))) * (rng.random(shape[:-2] + (1, shape[-1] // 4)) > 0.0625), 4, axis=-1).astype(np.float32)
    return mx_ref.flush(v.astype(BF))
PG, PW = 8, 64
def bare(d):
    d["sm"][:, :, 4 * PG:] = 0; d["gs"][:, :, 8:] = 0
    return d
def sizes(rng, d):
    for n in ("sm", "gs"): d[n] = mx_ref.flush((d[n].astype(np.float32) * np.exp2(rng.integers(-12, 13, (N, 1, 1))).astype(np.float32)).astype(BF))
    return d
def setup_inputs(rng):
    return bare({"pg": f(rng, N, 128 * PG, 4 * PW), "sm": f(rng, N, 128, 512), "gs": f(rng, N, 128, 512), "qw": f(rng, N, 128, 1024)})
def setup_inputs_ties(rng):
    d = setup_inputs(rng); v = d["sm"].reshape(N, 128, 128, 4).copy()
    for q in range(N):
        k = rng.integers(PG // 4 + 1, PG // 2 + 1); p = rng.permutation(PG)
        v[q][:, p[k:]] = v[q][:, p[np.arange(k, PG) % k]]
    d["sm"] = v.reshape(N, 128, 512)
    d = sizes(rng, d)
    for r in rng.permutation(N)[:2]: d["gs"][r][:, 4:8] = 0
    return d
def setup_inputs_last(rng):
    d = setup_inputs(rng); c = f(rng, 128, 4)
    for r in range(N):
        j = rng.integers(0, 2)
        d["gs"][r][:, 4 * j:4 * j + 4] = c
        d["sm"][r][:, 4 * PG - 4:4 * PG] = (c.astype(np.float32) * 2).astype(BF)
    return d
def setup_inputs_alike(rng):
    d = setup_inputs(rng); d["gs"] = np.stack([d["gs"][0]] * N); return d
def setup_inputs_below(rng):
    d = setup_inputs(rng)
    d["gs"] = np.abs(d["gs"].astype(np.float32)).astype(BF)
    d["sm"] = (-np.abs(d["sm"].astype(np.float32))).astype(BF)
    return bare(sizes(rng, d))
def setup_inputs_spread(rng):
    d = setup_inputs(rng); d["pg"] = wide(rng, N, 128 * PG, 4 * PW); d["sm"] = wide(rng, N, 128, 512); d["gs"] = wide(rng, N, 128, 512)
    return bare(d)
def check_inputs(d):
    b = []
    for r in range(N):
        if d["sm"][r][:, 4 * PG:].astype(np.float32).any(): b.append("sm")
        if d["gs"][r][:, 8:].astype(np.float32).any(): b.append("gs")
    return b
def reference(pg, sm, gs, qw):
    S = [mx_ref.quantize(t) for t in sm]; G = [mx_ref.quantize(t) for t in gs]
    y = np.zeros((N, 128, 2 * N * PW), np.float32); ch = np.zeros((N, 2, N), np.float32)
    for r in range(N):
        W = [mx_ref.quantize(qw[r][:, 512 * j:512 * j + 512]) for j in range(2)]
        for q in range(N):
            score = mx_ref.matmul(S[q], G[r])
            for j in range(2):
                c = int(np.argmax(score[:PG, j]))
                k = PW * (j * N + q)
                y[r][:, k:k + PW] = mx_ref.matmul(W[j], mx_ref.quantize(pg[q][128 * c:128 * c + 128]))
                ch[r, j, q] = c
    return {"y": y, "ch": ch}

@@ -1,0 +1,367 @@
+from concourse.bass import DstId, RemoteDMATransfer
+from concourse.mybir import dt, AluOpType, ActivationFunctionType
+
+N, PG, PW = 8, 8, 64
+E = 4 * PW
+F8, U8, F32, BF, I32 = "float8_e4m3fn_x4", "uint8", "float32", "bfloat16", "int32"
+SCRATCH = {
+    "gsb": ("sbuf", [128, 512], BF), "smr": ("sbuf", [128, 512], BF),
+    "pgw": ("sbuf", [128, PG * E], BF), "qwb": ("sbuf", [128, 1024], BF),
+    "grc": ("sbuf", [128, 144], F8), "grp": ("sbuf", [128, 144], U8),
+    "smc": ("sbuf", [128, 192], F8), "smp": ("sbuf", [128, 192], U8),
+    "wc": ("sbuf", [128, 256], F8), "wp": ("sbuf", [128, 256], U8),
+    "h": ("sbuf", [128, 8 * 512], BF),
+    "qc": ("sbuf", [128, 7 * 128], F8), "qp": ("sbuf", [128, 7 * 128], U8),
+    "lc": ("sbuf", [128, N * 128], F8), "lp": ("sbuf", [128, N * 128], U8),
+    "rgc": ("sbuf", [128, 2], F8), "rgp": ("sbuf", [128, 8], U8),
+    "rsc": ("sbuf", [128, 8], F8), "rsp": ("sbuf", [128, 32], U8),
+    "rpc": ("sbuf", [128, 256], F8), "rpp": ("sbuf", [128, 256], U8),
+    "zz": ("sbuf", [128, 64], F32), "rb": ("sbuf", [128, 64], F32), "wt": ("sbuf", [128, 64], F32),
+    "ta": ("sbuf", [128, 16], I32), "tb": ("sbuf", [128, 16], I32), "tc": ("sbuf", [128, 16], I32),
+    "base": ("sbuf", [128, 16], F32),
+    "pc": ("sbuf", [128, 64], F32), "ic": ("sbuf", [128, 64], F32), "jc": ("sbuf", [128, 64], F32),
+    "kc": ("sbuf", [128, 64], F32), "chs": ("sbuf", [128, 8], F32),
+    "ysb": ("sbuf", [128, 1024], F32),
+}
+for _b in "DX":
+    SCRATCH["ts" + _b] = ("sbuf", [128, 32], F32)
+    SCRATCH["pm" + _b] = ("sbuf", [128, 8], F32)
+    SCRATCH["ind" + _b] = ("sbuf", [128, 64], F32)
+    SCRATCH["cc" + _b] = ("sbuf", [128, 64], F32)
+    SCRATCH["ct" + _b] = ("sbuf", [128, 32], F32)
+    SCRATCH["off" + _b] = ("sbuf", [128, 128], "uint16")
+for _i in range(8):
+    SCRATCH["ps%d" % _i] = ("psum", [128, 512], F32)
+SEMAPHORES = (["ldg", "lds", "ldp", "ldw", "v0", "vg", "v1", "vs", "v2", "v3", "it", "lg", "gd", "gx", "sa",
+               "tD", "tX", "tC", "cD", "cX", "cC", "wq", "qda", "qdb", "qxa", "qxb", "qo",
+               "rg", "rs", "rp0", "rp1", "ls", "st", "sch"]
+              + ["%s%d" % (n, i) for n in ("fv", "fs", "hv", "hs", "pg", "ma", "mb", "yv", "ys") for i in range(8)])
+BIG = 1e29
+
+
+def relays(topo, rc, far):
+    c = [x for x in topo.cores_of(rc) if x != rc and all(topo.may_write(x, d) for d in far)]
+    near = [x for x in c if topo.die(x) == topo.die(rc)]
+    away = [x for x in c if topo.die(x) != topo.die(rc)]
+    return [near[0], away[0]], [near[1], away[1]]
+
+
+def classes(topo, cores, r):
+    same = [q for q in range(N) if q == r or topo.same_plane(cores[q], cores[r])]
+    return same, [q for q in range(N) if q not in same]
+
+
+def mask(es):
+    m = 0
+    for e in es:
+        m |= 1 << e
+    return m
+
+
+def rank_program(g, core, T, topo):
+    cores = T.cores
+    total, waited = {}, {}
+
+    def sem(n):
+        return T.sem[n]
+
+    def wait(eng, n, v):
+        eng.wait_ge(sem(n), v)
+        waited[n] = max(waited.get(n, 0), v)
+
+    def inc(inst, n, v=1):
+        inst.then_inc(sem(n), v)
+        total[n] = total.get(n, 0) + v
+
+    def fused(parts, ls="ls"):
+        tr = []
+        for src, dsts, es, s in parts:
+            ids = []
+            for d, _ in dsts:
+                rid, pid = topo.addr(d, core)
+                ids.append(DstId(rid=rid, pnc=pid))
+            tr.append(RemoteDMATransfer(dst_ids=ids, dma_engine_mask=mask(es), remote_sem=sem(s),
+                                        srcs=[src], dsts=[a for _, a in dsts]))
+            total[ls] = total.get(ls, 0) + len(es)
+        g.remote_dma_fused(tr, local_sem=sem(ls))
+
+    def send(src, d, dst, es, s):
+        rid, pid = topo.addr(d, core)
+        g.remote_dma(dst, src, sem(s), sem("ls"), pid, rid, mask(es))
+        total["ls"] = total.get("ls", 0) + len(es)
+
+    def cod(t, a, b):
+        return t[:, a:b].bitcast(dt.uint8)
+
+    def finish():
+        for n in total:
+            if waited.get(n, 0) < total[n]:
+                g.wait_ge(sem(n), total[n])
+
+    def sslot(q, d):
+        return 8 + 8 * (q if q < d else q - 1)
+
+    r = T.rank_of(core)
+    if r is None:
+        for q in range(N):
+            if core in topo.cores_of(cores[q]):
+                same, other = classes(topo, cores, q)
+                for b, rel in enumerate(relays(topo, cores[q], [cores[d] for d in other])):
+                    if core in rel:
+                        relay_part(g, T, topo, core, cores, q, same.index(q), other, rel.index(core), b, wait, fused, send, cod,
+                                   sslot)
+                        finish()
+        return
+
+    same, other = classes(topo, cores, r)
+    n4 = len(same)
+    s = same.index(r)
+    relc, relp = relays(topo, core, [cores[d] for d in other])
+    dD = [same[(s + 1 + k) % n4] for k in range(n4 - 1)]
+    off = topo.engines(core, cores[dD[0]])
+    far = [e for e in topo.engines(core, relc[0]) if e not in off]
+    hf = len(off) // 2
+    V, S, TE = g.vector, g.scalar, g.tensor
+    ADD, MAX, MIN, MUL = AluOpType.add, AluOpType.max, AluOpType.min, AluOpType.mult
+    LT, GT = AluOpType.is_lt, AluOpType.is_gt
+    CP = ActivationFunctionType.Copy
+
+    inc(g.sync.dma_start(T.gsb[:, 0:8], T.gs[:, 0:8]), "ldg", 16)
+    inc(S.dma_start(T.smr[:, 0:128], T.sm[:, 0:128]), "lds", 16)
+    for m in range(PG):
+        e = g.sync if m % 2 == 0 else S
+        inc(e.dma_start(T.pgw[:, E * m:E * m + E], T.pg[128 * m:128 * m + 128, :]), "ldp", 16)
+    wait(g.sync, "lg", 2 * hf)
+    inc(g.sync.dma_start(T.qwb[:], T.qw[:]), "ldw", 16)
+
+    inc(g.iota(T.ta[:], [[0, 16]], 0, 1), "it")
+    inc(g.iota(T.tb[:], [[16, 16]], 0, 0), "it")
+    inc(g.iota(T.wt[:], [[0, 8], [1, 8]], 0, 0, allow_small_or_imprecise_dtypes=True), "it")
+
+    wait(g, "vg", 1)
+    fused([(cod(T.grc, 16, 18), [(c, cod(T.rgc, 0, 2)) for c in relc], far[:hf], "rg"),
+           (T.grp[:, 16:24], [(c, T.rgp[:, 0:8]) for c in relp], far[hf:], "rg")], "lg")
+
+    def gslot(d):
+        return 10 + 2 * ((same.index(d) - s - 1) % n4)
+    fused([(cod(T.grc, 16, 18), [(cores[d], cod(T.grc, gslot(d), gslot(d) + 2)) for d in dD], off[:hf], "gd")])
+    fused([(T.grp[:, 16:18], [(cores[d], T.grp[:, gslot(d):gslot(d) + 2]) for d in dD], off[hf:], "gd")])
+    wait(g, "vs", 1)
+    fused([(cod(T.smc, 64, 72), [(c, cod(T.rsc, 0, 8)) for c in relc], far[:hf], "rs"),
+           (T.smp[:, 64:96], [(c, T.rsp[:, 0:32]) for c in relp], far[hf:], "rs")])
+    fused([(cod(T.smc, 64, 72), [(cores[d], cod(T.smc, sslot(r, d), sslot(r, d) + 8)) for d in dD], off[:hf], "sa")])
+    fused([(T.smp[:, 64:72], [(cores[d], T.smp[:, sslot(r, d):sslot(r, d) + 8]) for d in dD], off[hf:], "sa")])
+
+    def cq(k):
+        return cod(T.qc, 128 * k, 128 * k + 128)
+
+    def pq(k):
+        return T.qp[:, 128 * k:128 * k + 128]
+    lcd, lpd = cod(T.lc, 128 * r, 128 * r + 128), T.lp[:, 128 * r:128 * r + 128]
+    pn = "pg%d" % r
+    wait(g, "qda", 2)
+    fused([(cq(k), [(cores[dD[k]], lcd)], off[hf * k:hf * k + hf], pn) for k in range(2)])
+    fused([(pq(k), [(cores[dD[k]], lpd)], off[hf * k:hf * k + hf], pn) for k in range(2)])
+    for t in range(2):
+        wait(g, ("qxa", "qxb")[t], 2)
+        fused([(cq(3 + 2 * t + a), [(relc[a], cod(T.rpc, 128 * t, 128 * t + 128))], (off, far)[a], "rp%d" % t) for a in range(2)])
+        fused([(pq(3 + 2 * t + a), [(relp[a], T.rpp[:, 128 * t:128 * t + 128])], (off, far)[a], "rp%d" % t) for a in range(2)])
+    wait(g, "qdb", 1)
+    send(cq(2), cores[dD[2]], lcd, off, pn)
+    send(pq(2), cores[dD[2]], lpd, off, pn)
+
+    inc(V.memset(T.gsb[:, 8:512], 0.0), "v0")
+    for t in ("zz", "indD", "indX"):
+        inc(V.memset(T[t][:], 0.0), "v2")
+    wait(V, "v0", 1)
+    wait(V, "ldg", 16)
+    inc(V.quantize_mx(T.grc[:, 16:144], T.grp[:, 16:144], T.gsb[:]), "vg")
+    wait(V, "lds", 16)
+    inc(V.tensor_copy(T.smr[:, 128:256], T.smr[:, 0:128]), "v1")
+    wait(V, "v1", 1)
+    inc(V.tensor_copy(T.smr[:, 256:512], T.smr[:, 0:256]), "v1")
+    wait(V, "v1", 2)
+    inc(V.quantize_mx(T.smc[:, 64:192], T.smp[:, 64:192], T.smr[:]), "vs")
+    inc(V.memset(T.rb[:], BIG), "v2")
+    inc(V.memset(T.ic[:], 0.0), "v2")
+    wait(V, "it", 3)
+    inc(V.tensor_scalar(T.tc[:], T.ta[:], 15, None, AluOpType.bitwise_and), "v2")
+    wait(V, "v2", 6)
+    inc(V.memset(T.rb[:, 0:64:8], -BIG), "v3")
+    inc(V.tensor_tensor(T.base[:], T.tc[:], T.tb[:], ADD), "v3")
+    wait(V, "v3", 2)
+
+    def chain(b, ps):
+        c = "c" + b
+        wait(V, "t" + b, 1)
+        inc(V.transpose(T["ts" + b][:], T[ps][:, 0:32]), c)
+        wait(V, c, 1)
+        inc(V.tensor_tensor_scan(T["pm" + b][:], T.zz[:, 0:8], T["ts" + b][:, 0:8], -BIG, ADD, MAX), c)
+        wait(V, c, 2)
+        inc(V.tensor_scalar(T["ind" + b][:, 24:32], T["pm" + b][:], T["pm" + b][:, 7:8], float(E), LT, MUL), c)
+        wait(V, c, 3)
+        inc(V.tensor_tensor_scan(T["cc" + b][:, 24:64], T["ind" + b][:, 24:64], T.zz[:, 0:40], 0.0, ADD, ADD), c)
+        wait(V, c, 4)
+        inc(V.transpose(T["ct" + b][:], T["cc" + b][:, 32:64]), c)
+        wait(V, c, 5)
+
+    def offs(b, i, n):
+        inc(V.tensor_scalar(T["off" + b][:, 16 * i:16 * i + 16], T.base[:], T["ct" + b][:, i:i + 1], None, ADD), n)
+
+    def lists(b, i, d, eng):
+        for j in range(2):
+            offs(b, i + j, "f%s%d" % (eng, d))
+
+    def gather(eng, b, i, d, j, w):
+        out = T.h[:, 512 * d + E * j:512 * d + E * (j + w)]
+        win = T.pgw[:, 0:PG * E].indirect(T["off" + b][:, 16 * i:16 * (i + w)])
+        if eng == "V":
+            wait(V, "fv%d" % d, w)
+            inc(V.tensor_copy(out, win), "hv%d" % d)
+        else:
+            wait(S, "fs%d" % d, w)
+            inc(S.activation(out, win, CP), "hs%d" % d)
+
+    def quant(d, n):
+        o = (T.lc[:, 128 * r:128 * r + 128], T.lp[:, 128 * r:128 * r + 128]) if d == 7 else \
+            (T.qc[:, 128 * d:128 * d + 128], T.qp[:, 128 * d:128 * d + 128])
+        inc(V.quantize_mx(o[0], o[1], T.h[:, 512 * d:512 * d + 512]), n)
+
+    def pair(b, iv, dv, i2, d2, n):
+        gather("S", b, i2, d2, 0, 2)
+        gather("V", b, iv, dv, 0, 2)
+        wait(V, "hv%d" % dv, 1)
+        quant(dv, n)
+        wait(V, "hs%d" % d2, 1)
+        quant(d2, n)
+
+    def halves(b, i, d):
+        offs(b, i + 1, "fs%d" % d)
+        offs(b, i, "fv%d" % d)
+        gather("S", b, i + 1, d, 1, 1)
+        gather("V", b, i, d, 0, 1)
+
+    def done(d, n):
+        wait(V, "hv%d" % d, 1)
+        wait(V, "hs%d" % d, 1)
+        quant(d, n)
+
+    pe, ot = [same[(s - 1 - k) % n4] for k in range(n4 - 1)], [other[(s - k) % n4] for k in range(n4)]
+    order = pe[:2] + [r] + ot[:2] + pe[2:] + ot[2:]
+    banks = [(3, 4), (5, 6), (7, 0), (1, 2)]
+
+    def out(n):
+        a, b = PW * order[n], PW * (N + order[n])
+        pa, pb = (T["ps%d" % k] for k in banks[n % 4])
+        wait(S, "mb%d" % n, 1)
+        inc(S.activation(T.ysb[:, b:b + PW], pb[:, PW:2 * PW], CP), "ys%d" % n)
+        if n < 2:
+            wait(S, "ma%d" % n, 1)
+            inc(S.activation(T.ysb[:, a:a + PW], pa[:, 0:PW], CP), "yv%d" % n)
+        else:
+            wait(V, "ma%d" % n, 1)
+            inc(V.tensor_copy(T.ysb[:, a:a + PW], pa[:, 0:PW]), "yv%d" % n)
+
+    chain("D", "ps0")
+    cold = [2 * ((s - same.index(d) - 1) % n4) for d in dD]
+    lists("D", cold[1], 1, "s")
+    lists("D", cold[0], 0, "v")
+    wait(V, "ldp", 16 * PG)
+    wait(S, "ldp", 16 * PG)
+    pair("D", cold[0], 0, cold[1], 1, "qda")
+
+    chain("X", "ps1")
+    colx = [2 * ((s + k) % n4) for k in range(4)]
+    lists("X", colx[1], 4, "s")
+    lists("X", colx[0], 3, "v")
+    lists("X", colx[3], 6, "s")
+    pair("X", colx[0], 3, colx[1], 4, "qxa")
+    gather("S", "X", colx[3], 6, 0, 2)
+    halves("X", colx[2], 5)
+    wait(V, "hs6", 1)
+    quant(6, "qxb")
+    done(5, "qxb")
+    wait(V, "ldw", 16)
+    inc(V.quantize_mx(T.wc[:], T.wp[:], T.qwb[:]), "wq")
+    halves("D", cold[2], 2)
+    done(2, "qdb")
+
+    halves("D", 6, 7)
+    done(7, "qo")
+    wait(V, "tC", 1)
+    inc(V.tensor_tensor_scan(T.pc[0:2, :], T.rb[0:2, :], T.ps2[0:2, 0:64], 0.0, MIN, MAX), "cC")
+
+    def choices():
+        wait(V, "cC", 1)
+        inc(V.tensor_tensor(T.ic[0:2, 1:64], T.pc[0:2, 1:64], T.pc[0:2, 0:63], GT), "cC")
+        wait(V, "cC", 2)
+        inc(V.tensor_tensor(T.jc[0:2, :], T.ic[0:2, :], T.wt[0:2, :], MUL), "cC")
+        wait(V, "cC", 3)
+        inc(V.tensor_tensor_scan(T.kc[0:2, :], T.rb[0:2, :], T.jc[0:2, :], 0.0, MIN, MAX), "cC")
+        wait(V, "cC", 4)
+        if r > 0:
+            inc(V.tensor_copy(T.chs[0:2, 0:r], T.kc[0:2, 7:8 * r:8]), "sch")
+        if r < N - 1:
+            inc(V.tensor_copy(T.chs[0:2, r + 1:N], T.kc[0:2, 8 * r + 7:56:8]), "sch")
+        inc(V.tensor_copy(T.chs[0:2, r:r + 1], T.kc[0:2, 63:64]), "sch")
+
+    own = (T.smc[:, 64:192], T.smp[:, 64:192])
+    wait(TE, "vg", 1)
+    wait(TE, "vs", 1)
+    wait(TE, "gd", 2 * hf * (n4 - 1))
+    inc(TE.matmul_mx(T.ps0[:, 0:128], own[0], own[1], T.grc[:, 10:138], T.grp[:, 10:138], True, True), "tD")
+    wait(TE, "gx", 4 * hf * n4)
+    inc(TE.matmul_mx(T.ps1[:, 0:128], own[0], own[1], T.grc[:, 2:130], T.grp[:, 2:130], True, True), "tX")
+    wait(TE, "sa", 2 * hf * (n4 - 1) + 4 * hf * n4)
+    inc(TE.matmul_mx(T.ps2[:, 0:128], T.grc[:, 16:144], T.grp[:, 16:144], T.smc[:, 8:136], T.smp[:, 8:136], True, True), "tC")
+    wait(TE, "wq", 1)
+    held = order.index(pe[2])
+    for n in range(N):
+        q = order[n]
+        if q == r:
+            wait(TE, "qo", 1)
+        else:
+            wait(TE, "pg%d" % q, 2 * hf if q in pe[:2] else 4 * hf)
+        if n == 2:
+            wait(TE, "cD", 5)
+        if n == 3:
+            wait(TE, "cX", 5)
+            wait(TE, "cC", 1)
+        if n >= 4:
+            wait(TE, "yv%d" % (n - 4), 1)
+            wait(TE, "ys%d" % (n - 4), 1)
+        for j in (1, 0):
+            inc(TE.matmul_mx(T["ps%d" % banks[n % 4][j]][:, 0:128], T.wc[:, 128 * j:128 * j + 128], T.wp[:, 128 * j:128 * j + 128],
+                             T.lc[:, 128 * q:128 * q + 128], T.lp[:, 128 * q:128 * q + 128], True, True), "%s%d" % (("ma", "mb")[j], n))
+        out(n)
+        if n == 4:
+            choices()
+        if n != held:
+            ms = [held, n] if n == N - 1 else [n]
+            lo = PW * min(order[m] for m in ms)
+            for e, nm, a in ((S if n == N - 1 else g.sync, "ys", PW * N + lo), (g.sync, "yv", lo)):
+                for m in ms:
+                    wait(e, "%s%d" % (nm, m), 1)
+                b = a + PW * len(ms)
+                inc(e.dma_start(T.y[:, a:b], T.ysb[:, a:b]), "st", 16)
+        if n == 4:
+            wait(g.sync, "sch", total["sch"])
+            inc(g.sync.dma_start(T.ch[:], T.chs[0:2, :]), "st", 16)
+    finish()
+
+
+def relay_part(g, T, topo, core, cores, q, s, other, a, b, wait, fused, send, cod, sslot):
+    n4 = len(other)
+    dst = [other[(s + a + 2 * t) % n4] for t in range(2)]
+    es = topo.engines(core, cores[dst[0]])
+
+    def v(c, p, i, j):
+        return T[p][:, i:j] if b else cod(T[c], i, j)
+    wait(g, "rg", len(es) // 2)
+    k = 2 + 2 * s
+    fused([(v("rgc", "rgp", 0, 2), [(cores[d], v("grc", "grp", k, k + 2)) for d in dst], es, "gx")])
+    wait(g, "rs", len(es) // 2)
+    fused([(v("rsc", "rsp", 0, 8), [(cores[d], v("smc", "smp", sslot(q, d), sslot(q, d) + 8)) for d in dst], es, "sa")])
+    for t in range(2):
+        wait(g, "rp%d" % t, len(es))
+        send(v("rpc", "rpp", 128 * t, 128 * t + 128), cores[dst[t]], v("lc", "lp", 128 * q, 128 * q + 128), es, "pg%d" % q)

@@ -3,47 +3,51 @@ from concourse.mybir import dt, AluOpType, ActivationFunctionType
 
 N, PG, PW = 8, 8, 64
 E = 4 * PW
-F8, U8, F32, BF, I32 = "float8_e4m3fn_x4", "uint8", "float32", "bfloat16", "int32"
+ALL = PG * PW
+F8, U8, F32, BF, I32, U16 = "float8_e4m3fn_x4", "uint8", "float32", "bfloat16", "int32", "uint16"
 SCRATCH = {
     "gsb": ("sbuf", [128, 512], BF), "smr": ("sbuf", [128, 512], BF),
     "pgw": ("sbuf", [128, PG * E], BF), "qwb": ("sbuf", [128, 1024], BF),
     "grc": ("sbuf", [128, 144], F8), "grp": ("sbuf", [128, 144], U8),
     "smc": ("sbuf", [128, 192], F8), "smp": ("sbuf", [128, 192], U8),
-    "wc": ("sbuf", [128, 256], F8), "wp": ("sbuf", [128, 256], U8),
-    "h": ("sbuf", [128, 8 * 512], BF),
-    "qc": ("sbuf", [128, 7 * 128], F8), "qp": ("sbuf", [128, 7 * 128], U8),
+    "wc": ("sbuf", [128, 256], F8),
+    "fc": ("sbuf", [128, ALL], F8), "fp": ("sbuf", [128, ALL], U8),
+    "h": ("sbuf", [128, 5 * 512], BF),
+    "qc": ("sbuf", [128, 5 * 128], F8), "qp": ("sbuf", [128, 7 * 128], U8),
     "lc": ("sbuf", [128, N * 128], F8), "lp": ("sbuf", [128, N * 128], U8),
+    "lfc": ("sbuf", [128, 2 * ALL], F8), "lfp": ("sbuf", [128, 2 * ALL], U8), "lch": ("sbuf", [128, 4], F32),
     "rgc": ("sbuf", [128, 2], F8), "rgp": ("sbuf", [128, 8], U8),
     "rsc": ("sbuf", [128, 8], F8), "rsp": ("sbuf", [128, 32], U8),
-    "rpc": ("sbuf", [128, 256], F8), "rpp": ("sbuf", [128, 256], U8),
+    "rfc": ("sbuf", [128, 128], F8), "rfp": ("sbuf", [128, 128], U8), "rch": ("sbuf", [128, 2], F32),
+    "rpc": ("sbuf", [128, 128], F8), "rpp": ("sbuf", [128, 512], U8),
     "zz": ("sbuf", [128, 64], F32), "rb": ("sbuf", [128, 64], F32), "wt": ("sbuf", [128, 64], F32),
     "ta": ("sbuf", [128, 16], I32), "tb": ("sbuf", [128, 16], I32), "tc": ("sbuf", [128, 16], I32),
-    "base": ("sbuf", [128, 16], F32),
+    "base": ("sbuf", [128, 16], F32), "base4": ("sbuf", [128, 4], F32),
     "pc": ("sbuf", [128, 64], F32), "ic": ("sbuf", [128, 64], F32), "jc": ("sbuf", [128, 64], F32),
     "kc": ("sbuf", [128, 64], F32), "chs": ("sbuf", [128, 8], F32),
+    "off": ("sbuf", [128, 5 * 32], U16), "pk": ("sbuf", [128, 6 * 4], U16),
+    "fo": ("sbuf", [128, 6 * ALL], F32),
     "ysb": ("sbuf", [128, 1024], F32),
 }
 for _b in "DX":
-    SCRATCH["ts" + _b] = ("sbuf", [128, 32], F32)
-    SCRATCH["pm" + _b] = ("sbuf", [128, 8], F32)
-    SCRATCH["ind" + _b] = ("sbuf", [128, 64], F32)
-    SCRATCH["cc" + _b] = ("sbuf", [128, 64], F32)
-    SCRATCH["ct" + _b] = ("sbuf", [128, 32], F32)
-    SCRATCH["off" + _b] = ("sbuf", [128, 128], "uint16")
+    for _n, _w in (("ts", 32), ("pm", 8), ("ind", 64), ("cc", 64), ("ct", 32)):
+        SCRATCH[_n + _b] = ("sbuf", [128, _w], F32)
 for _i in range(8):
     SCRATCH["ps%d" % _i] = ("psum", [128, 512], F32)
-SEMAPHORES = (["ldg", "lds", "ldp", "ldw", "v0", "vg", "v1", "vs", "v2", "v3", "it", "lg", "gd", "gx", "sa",
-               "tD", "tX", "tC", "cD", "cX", "cC", "wq", "qda", "qdb", "qxa", "qxb", "qo",
-               "rg", "rs", "rp0", "rp1", "ls", "st", "sch"]
-              + ["%s%d" % (n, i) for n in ("fv", "fs", "hv", "hs", "pg", "ma", "mb", "yv", "ys") for i in range(8)])
+SEMAPHORES = (["ldg", "lds", "ldp", "ldw", "v0", "vg", "v1", "vs", "v2", "v3", "v4", "it", "gd", "gx", "sa", "tD", "tX", "tC",
+               "cD", "cX", "cC", "wq", "fq", "rg", "rs", "rf", "rq", "rc", "rp", "fa0", "fa1", "ca", "ls", "st", "sch"]
+              + ["%s%d" % (n, i) for n in ("fs", "hv", "hs", "qq", "ma", "mb") for i in range(5)]
+              + ["%s%d" % (n, i) for n in ("fm", "fk") for i in range(6)] + ["pl%d" % i for i in range(3)]
+              + ["%s%d" % (n, i) for n in ("pg", "yv", "ys") for i in range(8)])
 BIG = 1e29
+PAT = [256, 640, 768, 384, 512]
 
 
 def relays(topo, rc, far):
     c = [x for x in topo.cores_of(rc) if x != rc and all(topo.may_write(x, d) for d in far)]
     near = [x for x in c if topo.die(x) == topo.die(rc)]
     away = [x for x in c if topo.die(x) != topo.die(rc)]
-    return [near[0], away[0]], [near[1], away[1]]
+    return away[:2] + near[:2]
 
 
 def classes(topo, cores, r):
@@ -73,7 +77,7 @@ def rank_program(g, core, T, topo):
         inst.then_inc(sem(n), v)
         total[n] = total.get(n, 0) + v
 
-    def fused(parts, ls="ls"):
+    def fused(parts):
         tr = []
         for src, dsts, es, s in parts:
             ids = []
@@ -82,8 +86,8 @@ def rank_program(g, core, T, topo):
                 ids.append(DstId(rid=rid, pnc=pid))
             tr.append(RemoteDMATransfer(dst_ids=ids, dma_engine_mask=mask(es), remote_sem=sem(s),
                                         srcs=[src], dsts=[a for _, a in dsts]))
-            total[ls] = total.get(ls, 0) + len(es)
-        g.remote_dma_fused(tr, local_sem=sem(ls))
+            total["ls"] = total.get("ls", 0) + len(es)
+        g.remote_dma_fused(tr, local_sem=sem("ls"))
 
     def send(src, d, dst, es, s):
         rid, pid = topo.addr(d, core)
@@ -106,21 +110,22 @@ def rank_program(g, core, T, topo):
         for q in range(N):
             if core in topo.cores_of(cores[q]):
                 same, other = classes(topo, cores, q)
-                for b, rel in enumerate(relays(topo, cores[q], [cores[d] for d in other])):
-                    if core in rel:
-                        relay_part(g, T, topo, core, cores, q, same.index(q), other, rel.index(core), b, wait, fused, send, cod,
-                                   sslot)
-                        finish()
+                rel = relays(topo, cores[q], [cores[d] for d in other])
+                if core in rel:
+                    relay_part(g, T, topo, core, cores, q, same.index(q), other, rel.index(core), wait, fused, send, cod, sslot)
+                    finish()
         return
 
     same, other = classes(topo, cores, r)
     n4 = len(same)
     s = same.index(r)
-    relc, relp = relays(topo, core, [cores[d] for d in other])
+    rel = relays(topo, core, [cores[d] for d in other])
+    away, near = rel[:2], rel[2:]
     dD = [same[(s + 1 + k) % n4] for k in range(n4 - 1)]
     off = topo.engines(core, cores[dD[0]])
-    far = [e for e in topo.engines(core, relc[0]) if e not in off]
+    far = [e for e in topo.engines(core, rel[0]) if e not in off]
     hf = len(off) // 2
+    quads = [far[:hf], far[hf:], off[:hf], off[hf:]]
     V, S, TE = g.vector, g.scalar, g.tensor
     ADD, MAX, MIN, MUL = AluOpType.add, AluOpType.max, AluOpType.min, AluOpType.mult
     LT, GT = AluOpType.is_lt, AluOpType.is_gt
@@ -131,44 +136,49 @@ def rank_program(g, core, T, topo):
     for m in range(PG):
         e = g.sync if m % 2 == 0 else S
         inc(e.dma_start(T.pgw[:, E * m:E * m + E], T.pg[128 * m:128 * m + 128, :]), "ldp", 16)
-    wait(g.sync, "lg", 2 * hf)
     inc(g.sync.dma_start(T.qwb[:], T.qw[:]), "ldw", 16)
 
     inc(g.iota(T.ta[:], [[0, 16]], 0, 1), "it")
     inc(g.iota(T.tb[:], [[16, 16]], 0, 0), "it")
     inc(g.iota(T.wt[:], [[0, 8], [1, 8]], 0, 0, allow_small_or_imprecise_dtypes=True), "it")
 
-    wait(g, "vg", 1)
-    fused([(cod(T.grc, 16, 18), [(c, cod(T.rgc, 0, 2)) for c in relc], far[:hf], "rg"),
-           (T.grp[:, 16:24], [(c, T.rgp[:, 0:8]) for c in relp], far[hf:], "rg")], "lg")
-
     def gslot(d):
         return 10 + 2 * ((same.index(d) - s - 1) % n4)
-    fused([(cod(T.grc, 16, 18), [(cores[d], cod(T.grc, gslot(d), gslot(d) + 2)) for d in dD], off[:hf], "gd")])
-    fused([(T.grp[:, 16:18], [(cores[d], T.grp[:, gslot(d):gslot(d) + 2]) for d in dD], off[hf:], "gd")])
+    wait(g, "vg", 1)
+    fused([(cod(T.grc, 16, 18), [(c, cod(T.rgc, 0, 2)) for c in away], quads[0], "rg"),
+           (T.grp[:, 16:24], [(c, T.rgp[:]) for c in near], quads[1], "rg")])
+    fused([(cod(T.grc, 16, 18), [(cores[d], cod(T.grc, gslot(d), gslot(d) + 2)) for d in dD], quads[2], "gd")])
+    fused([(T.grp[:, 16:18], [(cores[d], T.grp[:, gslot(d):gslot(d) + 2]) for d in dD], quads[3], "gd")])
+    wait(g, "fq", 1)
+    fused([(T.fp[:, 128 * i:128 * i + 128], [(c, T.rfp[:])], quads[i], "rq") for i, c in enumerate(rel)])
+    fused([(cod(T.fc, 128 * i, 128 * i + 128), [(c, cod(T.rfc, 0, 128))], quads[i], "rf") for i, c in enumerate(rel)])
     wait(g, "vs", 1)
-    fused([(cod(T.smc, 64, 72), [(c, cod(T.rsc, 0, 8)) for c in relc], far[:hf], "rs"),
-           (T.smp[:, 64:96], [(c, T.rsp[:, 0:32]) for c in relp], far[hf:], "rs")])
-    fused([(cod(T.smc, 64, 72), [(cores[d], cod(T.smc, sslot(r, d), sslot(r, d) + 8)) for d in dD], off[:hf], "sa")])
-    fused([(T.smp[:, 64:72], [(cores[d], T.smp[:, sslot(r, d):sslot(r, d) + 8]) for d in dD], off[hf:], "sa")])
+    fused([(cod(T.smc, 64, 72), [(c, cod(T.rsc, 0, 8)) for c in away], quads[0], "rs"),
+           (T.smp[:, 64:96], [(c, T.rsp[:]) for c in near], quads[1], "rs")])
 
-    def cq(k):
-        return cod(T.qc, 128 * k, 128 * k + 128)
+    colx = [2 * ((s + k) % n4) for k in range(n4)]
+    score = [("ctD", 2 * ((s - same.index(d) - 1) % n4)) for d in dD] + [("ctX", c) for c in colx[2:]]
 
-    def pq(k):
-        return T.qp[:, 128 * k:128 * k + 128]
-    lcd, lpd = cod(T.lc, 128 * r, 128 * r + 128), T.lp[:, 128 * r:128 * r + 128]
-    pn = "pg%d" % r
-    wait(g, "qda", 2)
-    fused([(cq(k), [(cores[dD[k]], lcd)], off[hf * k:hf * k + hf], pn) for k in range(2)])
-    fused([(pq(k), [(cores[dD[k]], lpd)], off[hf * k:hf * k + hf], pn) for k in range(2)])
-    for t in range(2):
-        wait(g, ("qxa", "qxb")[t], 2)
-        fused([(cq(3 + 2 * t + a), [(relc[a], cod(T.rpc, 128 * t, 128 * t + 128))], (off, far)[a], "rp%d" % t) for a in range(2)])
-        fused([(pq(3 + 2 * t + a), [(relp[a], T.rpp[:, 128 * t:128 * t + 128])], (off, far)[a], "rp%d" % t) for a in range(2)])
-    wait(g, "qdb", 1)
-    send(cq(2), cores[dD[2]], lcd, off, pn)
-    send(pq(2), cores[dD[2]], lpd, off, pn)
+    def cq(d):
+        return cod(T.qc, 128 * d, 128 * d + 128)
+
+    def pq(d):
+        return T.qp[:, PAT[d]:PAT[d] + 128]
+
+    def to_peer(d):
+        wait(g, "qq%d" % d, 1)
+        send(cq(d), cores[dD[d]], cod(T.lc, 128 * r, 128 * r + 128), off, "pg%d" % r)
+        send(pq(d), cores[dD[d]], T.lp[:, 128 * r:128 * r + 128], off, "pg%d" % r)
+    wait(g, "cX", 5)
+    fused([(T.ctX[:, colx[k]:colx[k] + 2], [(near[k], T.rch[:])], quads[k], "rc") for k in range(2)])
+    to_peer(0)
+    wait(g, "wq", 1)
+    for a in range(2):
+        wait(g, "qq%d" % (3 + a), 1)
+        e = PAT[3 + a] + 128
+        fused([(cq(3 + a), [(away[a], cod(T.rpc, 0, 128))], far, "rp"), (T.qp[:, e - 512:e], [(near[a], T.rpp[:])], off, "rp")])
+    to_peer(1)
+    to_peer(2)
 
     inc(V.memset(T.gsb[:, 8:512], 0.0), "v0")
     for t in ("zz", "indD", "indX"):
@@ -190,106 +200,92 @@ def rank_program(g, core, T, topo):
     inc(V.memset(T.rb[:, 0:64:8], -BIG), "v3")
     inc(V.tensor_tensor(T.base[:], T.tc[:], T.tb[:], ADD), "v3")
     wait(V, "v3", 2)
+    inc(V.tensor_scalar(T.base4[:], T.base[:, 0:4], 4.0, None, MUL), "v4")
+    wait(V, "ldp", 16 * PG)
+    inc(V.quantize_mx(T.fc[:], T.fp[:], T.pgw[:]), "fq")
+    wait(V, "ldw", 16)
+    inc(V.quantize_mx(T.wc[:], T.qp[:, 0:256], T.qwb[:]), "wq")
+    wait(V, "v4", 1)
 
-    def chain(b, ps):
+    def chain(b, ps, between=()):
         c = "c" + b
+        ts, pm, ind, cc, ct = (T[n + b] for n in ("ts", "pm", "ind", "cc", "ct"))
+        steps = [lambda: V.transpose(ts[:], ps[:, 0:32]),
+                 lambda: V.tensor_tensor_scan(pm[:], T.zz[:, 0:8], ts[:, 0:8], -BIG, ADD, MAX),
+                 lambda: V.tensor_scalar(ind[:, 24:32], pm[:], pm[:, 7:8], float(E), LT, MUL),
+                 lambda: V.tensor_tensor_scan(cc[:, 24:64], ind[:, 24:64], T.zz[:, 0:40], 0.0, ADD, ADD),
+                 lambda: V.transpose(ct[:], cc[:, 32:64])]
         wait(V, "t" + b, 1)
-        inc(V.transpose(T["ts" + b][:], T[ps][:, 0:32]), c)
-        wait(V, c, 1)
-        inc(V.tensor_tensor_scan(T["pm" + b][:], T.zz[:, 0:8], T["ts" + b][:, 0:8], -BIG, ADD, MAX), c)
-        wait(V, c, 2)
-        inc(V.tensor_scalar(T["ind" + b][:, 24:32], T["pm" + b][:], T["pm" + b][:, 7:8], float(E), LT, MUL), c)
-        wait(V, c, 3)
-        inc(V.tensor_tensor_scan(T["cc" + b][:, 24:64], T["ind" + b][:, 24:64], T.zz[:, 0:40], 0.0, ADD, ADD), c)
-        wait(V, c, 4)
-        inc(V.transpose(T["ct" + b][:], T["cc" + b][:, 32:64]), c)
-        wait(V, c, 5)
+        for k, step in enumerate(steps):
+            inc(step(), c)
+            if k < len(between):
+                between[k]()
+            wait(V, c, k + 1)
 
-    def offs(b, i, n):
-        inc(V.tensor_scalar(T["off" + b][:, 16 * i:16 * i + 16], T.base[:], T["ct" + b][:, i:i + 1], None, ADD), n)
-
-    def lists(b, i, d, eng):
+    def lists(d):
+        t, c = score[d]
         for j in range(2):
-            offs(b, i + j, "f%s%d" % (eng, d))
+            i = 32 * d + 16 * j
+            inc(V.tensor_scalar(T.off[:, i:i + 16], T.base[:], T[t][:, c + j:c + j + 1], None, ADD), "fs%d" % d)
 
-    def gather(eng, b, i, d, j, w):
-        out = T.h[:, 512 * d + E * j:512 * d + E * (j + w)]
-        win = T.pgw[:, 0:PG * E].indirect(T["off" + b][:, 16 * i:16 * (i + w)])
-        if eng == "V":
-            wait(V, "fv%d" % d, w)
+    def gather(e, d, a, b):
+        out = T.h[:, 512 * d + 16 * a:512 * d + 16 * b]
+        win = T.pgw[:].indirect(T.off[:, 32 * d + a:32 * d + b])
+        wait(e, "fs%d" % d, 2)
+        if e is V:
             inc(V.tensor_copy(out, win), "hv%d" % d)
         else:
-            wait(S, "fs%d" % d, w)
             inc(S.activation(out, win, CP), "hs%d" % d)
 
-    def quant(d, n):
-        o = (T.lc[:, 128 * r:128 * r + 128], T.lp[:, 128 * r:128 * r + 128]) if d == 7 else \
-            (T.qc[:, 128 * d:128 * d + 128], T.qp[:, 128 * d:128 * d + 128])
-        inc(V.quantize_mx(o[0], o[1], T.h[:, 512 * d:512 * d + 512]), n)
-
-    def pair(b, iv, dv, i2, d2, n):
-        gather("S", b, i2, d2, 0, 2)
-        gather("V", b, iv, dv, 0, 2)
-        wait(V, "hv%d" % dv, 1)
-        quant(dv, n)
-        wait(V, "hs%d" % d2, 1)
-        quant(d2, n)
-
-    def halves(b, i, d):
-        offs(b, i + 1, "fs%d" % d)
-        offs(b, i, "fv%d" % d)
-        gather("S", b, i + 1, d, 1, 1)
-        gather("V", b, i, d, 0, 1)
-
-    def done(d, n):
-        wait(V, "hv%d" % d, 1)
-        wait(V, "hs%d" % d, 1)
-        quant(d, n)
+    def quant(d):
+        for n in ("hv%d" % d, "hs%d" % d):
+            if n in total:
+                wait(V, n, 1)
+        inc(V.quantize_mx(T.qc[:, 128 * d:128 * d + 128], pq(d), T.h[:, 512 * d:512 * d + 512]), "qq%d" % d)
 
     pe, ot = [same[(s - 1 - k) % n4] for k in range(n4 - 1)], [other[(s - k) % n4] for k in range(n4)]
-    order = pe[:2] + [r] + ot[:2] + pe[2:] + ot[2:]
-    banks = [(3, 4), (5, 6), (7, 0), (1, 2)]
+    whole, wbank = [r, ot[0], ot[1]], [5, 6, 3, 4, 5, 6]
+    order = [pe[0], pe[1], ot[2], pe[2], ot[3]]
+    banks = [(7, 0), (1, 2), (7, 0), (3, 4), (5, 6)]
+    stored = []
+
+    def drain(e, i):
+        wait(e, "fm%d" % i, 1)
+        a, b = T.fo[:, ALL * i:ALL * i + ALL], T["ps%d" % wbank[i]][:]
+        inc(V.tensor_copy(a, b) if e is V else S.activation(a, b, CP), "fk%d" % i)
+
+    def pick_lists(o, t, c):
+        for j in range(2):
+            i = 8 * o + 4 * j
+            inc(V.tensor_scalar(T.pk[:, i:i + 4], T.base4[:], t[:, c + j:c + j + 1], 0.25, ADD, MUL), "pl%d" % o)
+
+    def pick(o):
+        for j, e in enumerate((V, S)):
+            i, c = 2 * o + j, PW * (N * j + whole[o])
+            wait(e, "pl%d" % o, 2)
+            wait(e, "fk%d" % i, 1)
+            a, b = T.ysb[:, c:c + PW], T.fo[:, ALL * i:ALL * i + ALL].indirect(T.pk[:, 4 * i:4 * i + 4])
+            inc(S.activation(a, b, CP) if j else V.tensor_copy(a, b), "%s%d" % (("yv", "ys")[j], whole[o]))
+        store(whole[o])
 
     def out(n):
-        a, b = PW * order[n], PW * (N + order[n])
-        pa, pb = (T["ps%d" % k] for k in banks[n % 4])
+        q = order[n]
+        pa, pb = (T["ps%d" % k] for k in banks[n])
         wait(S, "mb%d" % n, 1)
-        inc(S.activation(T.ysb[:, b:b + PW], pb[:, PW:2 * PW], CP), "ys%d" % n)
-        if n < 2:
-            wait(S, "ma%d" % n, 1)
-            inc(S.activation(T.ysb[:, a:a + PW], pa[:, 0:PW], CP), "yv%d" % n)
-        else:
-            wait(V, "ma%d" % n, 1)
-            inc(V.tensor_copy(T.ysb[:, a:a + PW], pa[:, 0:PW]), "yv%d" % n)
+        inc(S.activation(T.ysb[:, PW * (N + q):PW * (N + q + 1)], pb[:, PW:2 * PW], CP), "ys%d" % q)
+        wait(V, "ma%d" % n, 1)
+        inc(V.tensor_copy(T.ysb[:, PW * q:PW * (q + 1)], pa[:, 0:PW]), "yv%d" % q)
+        store(q)
 
-    chain("D", "ps0")
-    cold = [2 * ((s - same.index(d) - 1) % n4) for d in dD]
-    lists("D", cold[1], 1, "s")
-    lists("D", cold[0], 0, "v")
-    wait(V, "ldp", 16 * PG)
-    wait(S, "ldp", 16 * PG)
-    pair("D", cold[0], 0, cold[1], 1, "qda")
-
-    chain("X", "ps1")
-    colx = [2 * ((s + k) % n4) for k in range(4)]
-    lists("X", colx[1], 4, "s")
-    lists("X", colx[0], 3, "v")
-    lists("X", colx[3], 6, "s")
-    pair("X", colx[0], 3, colx[1], 4, "qxa")
-    gather("S", "X", colx[3], 6, 0, 2)
-    halves("X", colx[2], 5)
-    wait(V, "hs6", 1)
-    quant(6, "qxb")
-    done(5, "qxb")
-    wait(V, "ldw", 16)
-    inc(V.quantize_mx(T.wc[:], T.wp[:], T.qwb[:]), "wq")
-    halves("D", cold[2], 2)
-    done(2, "qdb")
-
-    halves("D", 6, 7)
-    done(7, "qo")
-    wait(V, "tC", 1)
-    inc(V.tensor_tensor_scan(T.pc[0:2, :], T.rb[0:2, :], T.ps2[0:2, 0:64], 0.0, MIN, MAX), "cC")
+    def store(q):
+        stored.append(q)
+        mate = q + 1 - 2 * (q % 2)
+        if mate in stored:
+            lo = PW * min(q, mate)
+            for e, nm, a in ((S if len(stored) == N else g.sync, "ys", PW * N + lo), (g.sync, "yv", lo)):
+                for m in (mate, q):
+                    wait(e, "%s%d" % (nm, m), 1)
+                inc(e.dma_start(T.y[:, a:a + 2 * PW], T.ysb[:, a:a + 2 * PW]), "st", 16)
 
     def choices():
         wait(V, "cC", 1)
@@ -304,64 +300,97 @@ def rank_program(g, core, T, topo):
         if r < N - 1:
             inc(V.tensor_copy(T.chs[0:2, r + 1:N], T.kc[0:2, 8 * r + 7:56:8]), "sch")
         inc(V.tensor_copy(T.chs[0:2, r:r + 1], T.kc[0:2, 63:64]), "sch")
+        wait(g.sync, "sch", total["sch"])
+        inc(g.sync.dma_start(T.ch[:], T.chs[0:2, :]), "st", 16)
 
+    drain(S, 0)
+    drain(S, 1)
+    chain("D", T.ps0)
+    lists(0)
+    wait(S, "ldp", 16 * PG)
+    gather(S, 0, 0, 32)
+    chain("X", T.ps1, [lambda: lists(1), lambda: lists(2), lambda: pick_lists(0, T.ctD, 6)])
+    lists(3)
+    lists(4)
+    quant(0)
+    for d in (3, 4, 1, 2):
+        gather(S, d, 14, 32)
+        gather(V, d, 0, 14)
+        quant(d)
+
+    drain(S, 3)
+    drain(S, 2)
+    wait(V, "ca", 4 * hf)
+    for o in (1, 2):
+        pick_lists(o, T.lch, 2 * o - 2)
+    pick(0)
+    pick(1)
+    drain(S, 5)
+    drain(V, 4)
+    wait(V, "tC", 1)
+    inc(V.tensor_tensor_scan(T.pc[0:2, :], T.rb[0:2, :], T.ps2[0:2, 0:64], 0.0, MIN, MAX), "cC")
+    pick(2)
+    for n in range(len(order)):
+        out(n)
+        if n == 0:
+            choices()
+
+    def product(bank, j, c, p, lo, w, n):
+        inc(TE.matmul_mx(T["ps%d" % bank][:, 0:w], T.wc[:, 128 * j:128 * j + 128], T.qp[:, 128 * j:128 * j + 128],
+                         c[:, lo:lo + w], p[:, lo:lo + w], True, True), n)
     own = (T.smc[:, 64:192], T.smp[:, 64:192])
+    wait(TE, "fq", 1)
+    wait(TE, "wq", 1)
+    for j in range(2):
+        product(wbank[j], j, T.fc, T.fp, 0, ALL, "fm%d" % j)
     wait(TE, "vg", 1)
     wait(TE, "vs", 1)
     wait(TE, "gd", 2 * hf * (n4 - 1))
     inc(TE.matmul_mx(T.ps0[:, 0:128], own[0], own[1], T.grc[:, 10:138], T.grp[:, 10:138], True, True), "tD")
     wait(TE, "gx", 4 * hf * n4)
     inc(TE.matmul_mx(T.ps1[:, 0:128], own[0], own[1], T.grc[:, 2:130], T.grp[:, 2:130], True, True), "tX")
-    wait(TE, "sa", 2 * hf * (n4 - 1) + 4 * hf * n4)
+    for k in range(2):
+        wait(TE, "fa%d" % k, 3 * hf * len(rel))
+        for j in range(2):
+            if k:
+                wait(TE, "fk%d" % j, 1)
+            product(wbank[2 + 2 * k + j], j, T.lfc, T.lfp, ALL * k, ALL, "fm%d" % (2 + 2 * k + j))
+    wait(TE, "sa", 4 * hf * (N - 1))
     inc(TE.matmul_mx(T.ps2[:, 0:128], T.grc[:, 16:144], T.grp[:, 16:144], T.smc[:, 8:136], T.smp[:, 8:136], True, True), "tC")
-    wait(TE, "wq", 1)
-    held = order.index(pe[2])
-    for n in range(N):
-        q = order[n]
-        if q == r:
-            wait(TE, "qo", 1)
-        else:
-            wait(TE, "pg%d" % q, 2 * hf if q in pe[:2] else 4 * hf)
-        if n == 2:
-            wait(TE, "cD", 5)
-        if n == 3:
-            wait(TE, "cX", 5)
-            wait(TE, "cC", 1)
-        if n >= 4:
-            wait(TE, "yv%d" % (n - 4), 1)
-            wait(TE, "ys%d" % (n - 4), 1)
+    freed = [[("cD", 5)], [("cX", 5), ("cC", 1)], [("yv%d" % order[0], 1), ("ys%d" % order[0], 1)],
+             [("fk2", 1), ("fk3", 1)], [("fk4", 1), ("fk5", 1)]]
+    for n, q in enumerate(order):
+        wait(TE, "pg%d" % q, 4 * hf)
+        for w in freed[n]:
+            wait(TE, *w)
         for j in (1, 0):
-            inc(TE.matmul_mx(T["ps%d" % banks[n % 4][j]][:, 0:128], T.wc[:, 128 * j:128 * j + 128], T.wp[:, 128 * j:128 * j + 128],
-                             T.lc[:, 128 * q:128 * q + 128], T.lp[:, 128 * q:128 * q + 128], True, True), "%s%d" % (("ma", "mb")[j], n))
-        out(n)
-        if n == 4:
-            choices()
-        if n != held:
-            ms = [held, n] if n == N - 1 else [n]
-            lo = PW * min(order[m] for m in ms)
-            for e, nm, a in ((S if n == N - 1 else g.sync, "ys", PW * N + lo), (g.sync, "yv", lo)):
-                for m in ms:
-                    wait(e, "%s%d" % (nm, m), 1)
-                b = a + PW * len(ms)
-                inc(e.dma_start(T.y[:, a:b], T.ysb[:, a:b]), "st", 16)
-        if n == 4:
-            wait(g.sync, "sch", total["sch"])
-            inc(g.sync.dma_start(T.ch[:], T.chs[0:2, :]), "st", 16)
+            product(banks[n][j], j, T.lc, T.lp, 128 * q, 128, "%s%d" % (("ma", "mb")[j], n))
     finish()
 
 
-def relay_part(g, T, topo, core, cores, q, s, other, a, b, wait, fused, send, cod, sslot):
+def relay_part(g, T, topo, core, cores, q, s, other, i, wait, fused, send, cod, sslot):
     n4 = len(other)
-    dst = [other[(s + a + 2 * t) % n4] for t in range(2)]
-    es = topo.engines(core, cores[dst[0]])
+    a, b = i % 2, i // 2
+    asker = [cores[other[(s + k) % n4]] for k in range(n4)]
+    es = topo.engines(core, asker[0])
+    hf = len(es) // 2
 
-    def v(c, p, i, j):
-        return T[p][:, i:j] if b else cod(T[c], i, j)
-    wait(g, "rg", len(es) // 2)
+    def v(c, p, lo, hi):
+        return T[p][:, lo:hi] if b else cod(T[c], lo, hi)
+    wait(g, "rg", hf)
     k = 2 + 2 * s
-    fused([(v("rgc", "rgp", 0, 2), [(cores[d], v("grc", "grp", k, k + 2)) for d in dst], es, "gx")])
-    wait(g, "rs", len(es) // 2)
-    fused([(v("rsc", "rsp", 0, 8), [(cores[d], v("smc", "smp", sslot(q, d), sslot(q, d) + 8)) for d in dst], es, "sa")])
-    for t in range(2):
-        wait(g, "rp%d" % t, len(es))
-        send(v("rpc", "rpp", 128 * t, 128 * t + 128), cores[dst[t]], v("lc", "lp", 128 * q, 128 * q + 128), es, "pg%d" % q)
+    fused([(v("rgc", "rgp", 0, 2), [(d, v("grc", "grp", k, k + 2)) for d in asker[a::2]], es, "gx")])
+    at = [ALL * k + 128 * i for k in range(2)]
+    wait(g, "rq", hf)
+    fused([(T.rfp[:], [(asker[k], T.lfp[:, at[k]:at[k] + 128])], es[hf * k:hf * k + hf], "fa%d" % k) for k in range(2)])
+    wait(g, "rf", hf)
+    for k in range(2):
+        send(cod(T.rfc, 0, 128), asker[k], cod(T.lfc, at[k], at[k] + 128), es, "fa%d" % k)
+    wait(g, "rs", hf)
+    to = [d for d in range(N) if d != q and (d in other) == (a == 0)]
+    fused([(v("rsc", "rsp", 0, 8), [(cores[d], v("smc", "smp", sslot(q, d), sslot(q, d) + 8)) for d in to], es, "sa")])
+    if b:
+        wait(g, "rc", hf)
+        send(T.rch[:], asker[a], T.lch[:, 2 * a:2 * a + 2], es, "ca")
+    wait(g, "rp", len(es))
+    send(v("rpc", "rpp", 384 * b, 384 * b + 128), asker[2 + a], v("lc", "lp", 128 * q, 128 * q + 128), es, "pg%d" % q)

@@ -4,55 +4,88 @@ from concourse.mybir import dt, AluOpType, ActivationFunctionType
 N, PG, PW = 8, 8, 64
 E = 4 * PW
 ALL = PG * PW
+NW = 3
+QCUT = [0, 192, 384, 512]
+CUT = [0, 166, 340, 512]
+PC = CUT[1] + PG
+LO = [-PG, CUT[1], ALL - PC]
+SP, FP = 144, 272
+XP = FP + ALL
+DOOR = {1: 1, 3: 2, 2: 2}
+HAND = [[0, 1, 2], [0, 2, 1], [0, 2, 1], [2, 0, 1]]
+LAST = (1, 3)
+SHARE = [0, 12, 12, 14]
+
+VECTOR = "l0 l1 X l3 q0 g3 l2 q3 g1 q1 g2 q2 d2 L d4 p2 p4 o00 d6 o10 p6 o30 o20"
+SCALAR = "p0 p1 g0 g3 g1 g2 d3 d5 p3 p5 o01 d7 o11 p7 o31 o21"
+TENSOR = "w0 w1 c0 w2 c1 c3 c2"
+SERVED = [0, 3, 1, 2]
+STORES = ["r w0", "c0 w1", "c1 w2", "c2 c3"]
+BANKS = {"w0": (4, 5), "w1": (6, 7), "w2": (0, 1), "c0": (2, 3), "c1": (4, 5), "c2": (2, 3), "c3": (6, 7)}
+
 F8, U8, F32, BF, I32, U16 = "float8_e4m3fn_x4", "uint8", "float32", "bfloat16", "int32", "uint16"
 SCRATCH = {
     "gsb": ("sbuf", [128, 512], BF), "smr": ("sbuf", [128, 512], BF),
     "pgw": ("sbuf", [128, PG * E], BF), "qwb": ("sbuf", [128, 1024], BF),
-    "grc": ("sbuf", [128, 144], F8), "grp": ("sbuf", [128, 144], U8),
-    "smc": ("sbuf", [128, 192], F8), "smp": ("sbuf", [128, 192], U8),
+    "grc": ("sbuf", [128, 144], F8),
+    "grp": ("sbuf", [128, XP + 128], U8),
+    "fc": ("sbuf", [128, 128 + ALL], F8),
     "wc": ("sbuf", [128, 256], F8),
-    "fc": ("sbuf", [128, ALL], F8), "fp": ("sbuf", [128, ALL], U8),
-    "h": ("sbuf", [128, 5 * 512], BF),
-    "qc": ("sbuf", [128, 5 * 128], F8), "qp": ("sbuf", [128, 7 * 128], U8),
+    "h": ("sbuf", [128, 4 * 512], BF),
+    "qc": ("sbuf", [128, 4 * 128], F8), "qp": ("sbuf", [128, 5 * 128], U8),
     "lc": ("sbuf", [128, N * 128], F8), "lp": ("sbuf", [128, N * 128], U8),
-    "lfc": ("sbuf", [128, 2 * ALL], F8), "lfp": ("sbuf", [128, 2 * ALL], U8), "lch": ("sbuf", [128, 4], F32),
+    "lfc": ("sbuf", [128, NW * ALL], F8), "lfp": ("sbuf", [128, NW * ALL], U8),
+    "lpk": ("sbuf", [128, 2 * NW], U16), "lch": ("sbuf", [128, 2], F32),
     "rgc": ("sbuf", [128, 2], F8), "rgp": ("sbuf", [128, 8], U8),
     "rsc": ("sbuf", [128, 8], F8), "rsp": ("sbuf", [128, 32], U8),
-    "rfc": ("sbuf", [128, 128], F8), "rfp": ("sbuf", [128, 128], U8), "rch": ("sbuf", [128, 2], F32),
+    "rfc": ("sbuf", [128, PC], F8), "rfp": ("sbuf", [128, 4 * PC], U8),
     "rpc": ("sbuf", [128, 128], F8), "rpp": ("sbuf", [128, 512], U8),
-    "zz": ("sbuf", [128, 64], F32), "rb": ("sbuf", [128, 64], F32), "wt": ("sbuf", [128, 64], F32),
+    "egc": ("sbuf", [128, 272], F8), "egp": ("sbuf", [128, 272], U8),
+    "esc": ("sbuf", [128, 320], F8), "esp": ("sbuf", [128, 320], U8),
+    "rb": ("sbuf", [128, 40], F32), "wt": ("sbuf", [128, 40], F32), "c16": ("sbuf", [128, 32], F32),
+    "sp": ("sbuf", [128, 32 * NW], F32), "st": ("sbuf", [128, 32 * NW], F32), "mpk": ("sbuf", [128, 2 * NW], U16),
+    "kq": ("sbuf", [128, 32], F32), "kt": ("sbuf", [128, 32], F32),
+    "zz": ("sbuf", [128, 64], F32),
     "ta": ("sbuf", [128, 16], I32), "tb": ("sbuf", [128, 16], I32), "tc": ("sbuf", [128, 16], I32),
     "base": ("sbuf", [128, 16], F32), "base4": ("sbuf", [128, 4], F32),
-    "pc": ("sbuf", [128, 64], F32), "ic": ("sbuf", [128, 64], F32), "jc": ("sbuf", [128, 64], F32),
-    "kc": ("sbuf", [128, 64], F32), "chs": ("sbuf", [128, 8], F32),
-    "off": ("sbuf", [128, 5 * 32], U16), "pk": ("sbuf", [128, 6 * 4], U16),
-    "fo": ("sbuf", [128, 6 * ALL], F32),
+    "off": ("sbuf", [128, 4 * 32], U16), "pk": ("sbuf", [128, 8 * 4], U16),
+    "fo": ("sbuf", [128, 8 * ALL], F32),
     "ysb": ("sbuf", [128, 1024], F32),
 }
-for _b in "DX":
+for _b in "ODX":
     for _n, _w in (("ts", 32), ("pm", 8), ("ind", 64), ("cc", 64), ("ct", 32)):
+        SCRATCH[_n + _b] = ("sbuf", [128, _w], F32)
+for _b, _w in (("D", 40), ("X", 24)):
+    for _n in ("pc", "ic", "jc", "kc"):
         SCRATCH[_n + _b] = ("sbuf", [128, _w], F32)
 for _i in range(8):
     SCRATCH["ps%d" % _i] = ("psum", [128, 512], F32)
-SEMAPHORES = (["ldg", "lds", "ldp", "ldw", "v0", "vg", "v1", "vs", "v2", "v3", "v4", "it", "gd", "gx", "sa", "tD", "tX", "tC",
-               "cD", "cX", "cC", "wq", "fq", "rg", "rs", "rf", "rq", "rc", "rp", "fa0", "fa1", "ca", "ls", "st", "sch"]
-              + ["%s%d" % (n, i) for n in ("fs", "hv", "hs", "qq", "ma", "mb") for i in range(5)]
-              + ["%s%d" % (n, i) for n in ("fm", "fk") for i in range(6)] + ["pl%d" % i for i in range(3)]
-              + ["%s%d" % (n, i) for n in ("pg", "yv", "ys") for i in range(8)])
+SEMAPHORES = (["ldg", "lds", "ldw", "v0", "vg", "v1", "vs", "v2", "v3", "v4", "v5", "it", "gd", "gx", "tO", "tD", "tX", "cO", "cD",
+               "cX", "wq", "rg", "rs", "rf", "rq", "rp", "eg", "sD", "sX", "em", "mp", "mc", "pl0", "pl1", "ls", "st"]
+              + ["%s%d" % (n, i) for n in ("ldp", "fq", "fa") for i in range(3)]
+              + ["%s%d" % (n, i) for n in ("fs", "hv", "hs", "qq", "m0", "m1") for i in range(4)]
+              + ["%s%d" % (n, i) for n in ("fm", "fk", "pg", "y0", "y1") for i in range(8)])
 BIG = 1e29
-PAT = [256, 640, 768, 384, 512]
-
-
-def relays(topo, rc, far):
-    c = [x for x in topo.cores_of(rc) if x != rc and all(topo.may_write(x, d) for d in far)]
-    near = [x for x in c if topo.die(x) == topo.die(rc)]
-    away = [x for x in c if topo.die(x) != topo.die(rc)]
-    return away[:2] + near[:2]
+ADD, MAX, MIN, MUL = AluOpType.add, AluOpType.max, AluOpType.min, AluOpType.mult
+LT, GT = AluOpType.is_lt, AluOpType.is_gt
 
 
 def classes(topo, cores, r):
     same = [q for q in range(N) if q == r or topo.same_plane(cores[q], cores[r])]
     return same, [q for q in range(N) if q not in same]
+
+
+def helpers(topo, cores, r):
+    rc, far = cores[r], [cores[d] for d in classes(topo, cores, r)[1]]
+    c = [x for x in topo.cores_of(rc) if x != rc]
+    rel = [x for x in c if all(topo.may_write(x, d) for d in far)]
+    near = [x for x in c if topo.die(x) == topo.die(rc)]
+    return [x for x in rel if x not in near] + [x for x in rel if x in near], [x for x in c if x not in rel and x not in near]
+
+
+def doors(topo, rc):
+    c = [x for x in range(256) if topo.mates(x, rc) and topo.may_write(x, rc)]
+    return [x for x in c if topo.die(x) != topo.die(rc)] + [x for x in c if topo.die(x) == topo.die(rc)]
 
 
 def mask(es):
@@ -62,19 +95,26 @@ def mask(es):
     return m
 
 
+def cod(t, a, b):
+    return t[:, a:b].bitcast(dt.uint8)
+
+
+def piece_of(T, i, k):
+    if k is None:
+        return cod(T.rfc, CUT[i] - LO[i], CUT[i + 1] - LO[i]) if i < 3 else T.rfp[:, 4 * PC - ALL:4 * PC]
+    return cod(T.lfc, ALL * k + CUT[i], ALL * k + CUT[i + 1]) if i < 3 else T.lfp[:, ALL * k:ALL * k + ALL]
+
+
 def rank_program(g, core, T, topo):
     cores = T.cores
     total, waited = {}, {}
 
-    def sem(n):
-        return T.sem[n]
-
     def wait(eng, n, v):
-        eng.wait_ge(sem(n), v)
+        eng.wait_ge(T.sem[n], v)
         waited[n] = max(waited.get(n, 0), v)
 
     def inc(inst, n, v=1):
-        inst.then_inc(sem(n), v)
+        inst.then_inc(T.sem[n], v)
         total[n] = total.get(n, 0) + v
 
     def fused(parts):
@@ -84,313 +124,363 @@ def rank_program(g, core, T, topo):
             for d, _ in dsts:
                 rid, pid = topo.addr(d, core)
                 ids.append(DstId(rid=rid, pnc=pid))
-            tr.append(RemoteDMATransfer(dst_ids=ids, dma_engine_mask=mask(es), remote_sem=sem(s),
+            tr.append(RemoteDMATransfer(dst_ids=ids, dma_engine_mask=mask(es), remote_sem=T.sem[s],
                                         srcs=[src], dsts=[a for _, a in dsts]))
             total["ls"] = total.get("ls", 0) + len(es)
-        g.remote_dma_fused(tr, local_sem=sem("ls"))
+        g.remote_dma_fused(tr, local_sem=T.sem["ls"])
 
     def send(src, d, dst, es, s):
         rid, pid = topo.addr(d, core)
-        g.remote_dma(dst, src, sem(s), sem("ls"), pid, rid, mask(es))
+        g.remote_dma(dst, src, T.sem[s], T.sem["ls"], pid, rid, mask(es))
         total["ls"] = total.get("ls", 0) + len(es)
 
-    def cod(t, a, b):
-        return t[:, a:b].bitcast(dt.uint8)
+    calls = (wait, inc, fused, send)
+    for r in range(N):
+        if topo.mates(core, cores[r]) and core in doors(topo, cores[r]):
+            door_part(g, T, topo, core, r, calls)
+        if core in topo.cores_of(cores[r]):
+            rel, carry = helpers(topo, cores, r)
+            if core == cores[r]:
+                rank_part(g, T, topo, r, calls)
+            elif core in rel:
+                relay_part(g, T, topo, core, r, calls)
+            elif core in carry:
+                carrier_part(g, T, topo, core, r, calls)
+    for n in total:
+        if waited.get(n, 0) < total[n]:
+            g.wait_ge(T.sem[n], total[n])
 
-    def finish():
-        for n in total:
-            if waited.get(n, 0) < total[n]:
-                g.wait_ge(sem(n), total[n])
 
-    def sslot(q, d):
-        return 8 + 8 * (q if q < d else q - 1)
-
-    r = T.rank_of(core)
-    if r is None:
-        for q in range(N):
-            if core in topo.cores_of(cores[q]):
-                same, other = classes(topo, cores, q)
-                rel = relays(topo, cores[q], [cores[d] for d in other])
-                if core in rel:
-                    relay_part(g, T, topo, core, cores, q, same.index(q), other, rel.index(core), wait, fused, send, cod, sslot)
-                    finish()
-        return
-
+def rank_part(g, T, topo, r, calls):
+    wait, inc, fused, send = calls
+    cores = T.cores
+    core = cores[r]
     same, other = classes(topo, cores, r)
+    rel, carry = helpers(topo, cores, r)
     n4 = len(same)
     s = same.index(r)
-    rel = relays(topo, core, [cores[d] for d in other])
-    away, near = rel[:2], rel[2:]
     dD = [same[(s + 1 + k) % n4] for k in range(n4 - 1)]
     off = topo.engines(core, cores[dD[0]])
     far = [e for e in topo.engines(core, rel[0]) if e not in off]
     hf = len(off) // 2
-    quads = [far[:hf], far[hf:], off[:hf], off[hf:]]
+    quads = [far[0::2], far[1::2], off[0::2], off[1::2]]
     V, S, TE = g.vector, g.scalar, g.tensor
-    ADD, MAX, MIN, MUL = AluOpType.add, AluOpType.max, AluOpType.min, AluOpType.mult
-    LT, GT = AluOpType.is_lt, AluOpType.is_gt
     CP = ActivationFunctionType.Copy
 
     inc(g.sync.dma_start(T.gsb[:, 0:8], T.gs[:, 0:8]), "ldg", 16)
-    inc(S.dma_start(T.smr[:, 0:128], T.sm[:, 0:128]), "lds", 16)
-    for m in range(PG):
-        e = g.sync if m % 2 == 0 else S
-        inc(e.dma_start(T.pgw[:, E * m:E * m + E], T.pg[128 * m:128 * m + 128, :]), "ldp", 16)
+    inc(S.dma_start(T.smr[:, 96:128], T.sm[:, 0:32]), "lds", 16)
+    part = [[m for m in range(PG) if QCUT[i] <= PW * m < QCUT[i + 1]] for i in range(3)]
+    for i in range(3):
+        for m in part[i]:
+            e = g.sync if m % 2 == 0 else S
+            inc(e.dma_start(T.pgw[:, E * m:E * m + E], T.pg[128 * m:128 * m + 128, :]), "ldp%d" % i, 16)
     inc(g.sync.dma_start(T.qwb[:], T.qw[:]), "ldw", 16)
 
     inc(g.iota(T.ta[:], [[0, 16]], 0, 1), "it")
     inc(g.iota(T.tb[:], [[16, 16]], 0, 0), "it")
-    inc(g.iota(T.wt[:], [[0, 8], [1, 8]], 0, 0, allow_small_or_imprecise_dtypes=True), "it")
-
-    def gslot(d):
-        return 10 + 2 * ((same.index(d) - s - 1) % n4)
+    slot = [(cores[dD[k]], 10 + 2 * k) for k in (1, 2)]
     wait(g, "vg", 1)
-    fused([(cod(T.grc, 16, 18), [(c, cod(T.rgc, 0, 2)) for c in away], quads[0], "rg"),
-           (T.grp[:, 16:24], [(c, T.rgp[:]) for c in near], quads[1], "rg")])
-    fused([(cod(T.grc, 16, 18), [(cores[d], cod(T.grc, gslot(d), gslot(d) + 2)) for d in dD], quads[2], "gd")])
-    fused([(T.grp[:, 16:18], [(cores[d], T.grp[:, gslot(d):gslot(d) + 2]) for d in dD], quads[3], "gd")])
-    wait(g, "fq", 1)
-    fused([(T.fp[:, 128 * i:128 * i + 128], [(c, T.rfp[:])], quads[i], "rq") for i, c in enumerate(rel)])
-    fused([(cod(T.fc, 128 * i, 128 * i + 128), [(c, cod(T.rfc, 0, 128))], quads[i], "rf") for i, c in enumerate(rel)])
+    fused([(cod(T.grc, 16, 18), [(a, cod(T.rgc, 0, 2)) for a in rel[0::2]], quads[0], "rg"),
+           (T.grp[:, 16:24], [(a, T.rgp[:]) for a in rel[1::2]], quads[1], "rg"),
+           (cod(T.grc, 16, 18), [(d, cod(T.grc, a, a + 2)) for d, a in slot], quads[2], "gd")])
+    fused([(T.grp[:, 16:18], [(d, T.grp[:, a:a + 2]) for d, a in slot], quads[3], "gd")])
     wait(g, "vs", 1)
-    fused([(cod(T.smc, 64, 72), [(c, cod(T.rsc, 0, 8)) for c in away], quads[0], "rs"),
-           (T.smp[:, 64:96], [(c, T.rsp[:]) for c in near], quads[1], "rs")])
-
-    colx = [2 * ((s + k) % n4) for k in range(n4)]
-    score = [("ctD", 2 * ((s - same.index(d) - 1) % n4)) for d in dD] + [("ctX", c) for c in colx[2:]]
+    for i in range(3):
+        wait(g, "fq%d" % i, 1)
+    runs = [cod(T.fc, 128 + LO[i], 128 + LO[i] + PC) for i in range(3)] + [T.grp[:, XP - 4 * PC:XP]]
+    fused([(runs[i], [(rel[i], cod(T.rfc, 0, PC) if i < 3 else T.rfp[:])], quads[(0, 2, 3, 1)[i]], "rf") for i in range(4)])
+    door = doors(topo, cores[other[(s + NW) % n4]])
+    smc, smp = cod(T.fc, 128 - PG, 128), T.grp[:, FP - 32:FP]
+    fused([(smc, [(carry[0], cod(T.esc, 160 + 8 * s, 168 + 8 * s))], quads[0], "rs"), (smp, [(carry[1], T.rsp[:])], quads[1], "rs"),
+           (smc, [(door[1], cod(T.rsc, 0, PG))], quads[2], "rs"), (smp, [(door[2], T.rsp[:])], quads[3], "rs")])
 
     def cq(d):
         return cod(T.qc, 128 * d, 128 * d + 128)
 
     def pq(d):
-        return T.qp[:, PAT[d]:PAT[d] + 128]
-
-    def to_peer(d):
+        return T.qp[:, 256 + 128 * d:384 + 128 * d] if d < 3 else T.grp[:, XP:XP + 128]
+    for d in SERVED:
         wait(g, "qq%d" % d, 1)
-        send(cq(d), cores[dD[d]], cod(T.lc, 128 * r, 128 * r + 128), off, "pg%d" % r)
-        send(pq(d), cores[dD[d]], T.lp[:, 128 * r:128 * r + 128], off, "pg%d" % r)
-    wait(g, "cX", 5)
-    fused([(T.ctX[:, colx[k]:colx[k] + 2], [(near[k], T.rch[:])], quads[k], "rc") for k in range(2)])
-    to_peer(0)
-    wait(g, "wq", 1)
-    for a in range(2):
-        wait(g, "qq%d" % (3 + a), 1)
-        e = PAT[3 + a] + 128
-        fused([(cq(3 + a), [(away[a], cod(T.rpc, 0, 128))], far, "rp"), (T.qp[:, e - 512:e], [(near[a], T.rpp[:])], off, "rp")])
-    to_peer(1)
-    to_peer(2)
+        if d < 3:
+            send(cq(d), cores[dD[d]], cod(T.lc, 128 * r, 128 * r + 128), off, "pg%d" % r)
+            fused([(pq(d), [(cores[dD[d]], T.lp[:, 128 * r:128 * r + 128])], off, "pg%d" % r)])
+        else:
+            fused([(cq(d), [(rel[LAST[0]], cod(T.rpc, 0, 128))], far, "rp"),
+                   (T.grp[:, XP - 384:XP + 128], [(rel[LAST[1]], T.rpp[:])], off, "rp")])
 
     inc(V.memset(T.gsb[:, 8:512], 0.0), "v0")
-    for t in ("zz", "indD", "indX"):
+    inc(V.memset(T.smr[:, 0:96], 0.0), "v5")
+    for t in ("zz", "indO", "indD", "indX"):
         inc(V.memset(T[t][:], 0.0), "v2")
     wait(V, "v0", 1)
     wait(V, "ldg", 16)
     inc(V.quantize_mx(T.grc[:, 16:144], T.grp[:, 16:144], T.gsb[:]), "vg")
     wait(V, "lds", 16)
+    wait(V, "v5", 1)
     inc(V.tensor_copy(T.smr[:, 128:256], T.smr[:, 0:128]), "v1")
+    wait(V, "it", 2)
+    inc(V.tensor_scalar(T.tc[:], T.ta[:], 15, None, AluOpType.bitwise_and), "v2")
     wait(V, "v1", 1)
     inc(V.tensor_copy(T.smr[:, 256:512], T.smr[:, 0:256]), "v1")
-    wait(V, "v1", 2)
-    inc(V.quantize_mx(T.smc[:, 64:192], T.smp[:, 64:192], T.smr[:]), "vs")
-    inc(V.memset(T.rb[:], BIG), "v2")
-    inc(V.memset(T.ic[:], 0.0), "v2")
-    wait(V, "it", 3)
-    inc(V.tensor_scalar(T.tc[:], T.ta[:], 15, None, AluOpType.bitwise_and), "v2")
-    wait(V, "v2", 6)
-    inc(V.memset(T.rb[:, 0:64:8], -BIG), "v3")
+    wait(V, "v2", 5)
     inc(V.tensor_tensor(T.base[:], T.tc[:], T.tb[:], ADD), "v3")
-    wait(V, "v3", 2)
+    wait(V, "v1", 2)
+    inc(V.quantize_mx(T.fc[:, 0:128], T.grp[:, SP:FP], T.smr[:]), "vs")
+    wait(V, "v3", 1)
     inc(V.tensor_scalar(T.base4[:], T.base[:, 0:4], 4.0, None, MUL), "v4")
-    wait(V, "ldp", 16 * PG)
-    inc(V.quantize_mx(T.fc[:], T.fp[:], T.pgw[:]), "fq")
+    for i in range(3):
+        wait(V, "ldp%d" % i, 16 * len(part[i]))
+        a, b = QCUT[i], QCUT[i + 1]
+        inc(V.quantize_mx(T.fc[:, 128 + a:128 + b], T.grp[:, FP + a:FP + b], T.pgw[:, 4 * a:4 * b]), "fq%d" % i)
     wait(V, "ldw", 16)
     inc(V.quantize_mx(T.wc[:], T.qp[:, 0:256], T.qwb[:]), "wq")
     wait(V, "v4", 1)
 
-    def chain(b, ps, between=()):
+    pe, ot = [same[(s - 1 - k) % n4] for k in range(n4 - 1)], [other[(s - k) % n4] for k in range(n4)]
+    whole, chosen = [r] + ot[:NW], pe + ot[NW:]
+    wbank = [0, 1] + [b for k in range(NW) for b in BANKS["w%d" % k]]
+    score = [("ctD", 2), ("ctD", 0), ("ctX", 2), ("ctX", 0)]
+
+    def chain(b, ps):
         c = "c" + b
         ts, pm, ind, cc, ct = (T[n + b] for n in ("ts", "pm", "ind", "cc", "ct"))
         steps = [lambda: V.transpose(ts[:], ps[:, 0:32]),
-                 lambda: V.tensor_tensor_scan(pm[:], T.zz[:, 0:8], ts[:, 0:8], -BIG, ADD, MAX),
+                 lambda: V.tensor_tensor_scan(pm[:], T.zz[:, 0:8], ts[:, 24:32], -BIG, ADD, MAX),
                  lambda: V.tensor_scalar(ind[:, 24:32], pm[:], pm[:, 7:8], float(E), LT, MUL),
                  lambda: V.tensor_tensor_scan(cc[:, 24:64], ind[:, 24:64], T.zz[:, 0:40], 0.0, ADD, ADD),
                  lambda: V.transpose(ct[:], cc[:, 32:64])]
         wait(V, "t" + b, 1)
         for k, step in enumerate(steps):
             inc(step(), c)
-            if k < len(between):
-                between[k]()
             wait(V, c, k + 1)
 
-    def lists(d):
-        t, c = score[d]
-        for j in range(2):
-            i = 32 * d + 16 * j
-            inc(V.tensor_scalar(T.off[:, i:i + 16], T.base[:], T[t][:, c + j:c + j + 1], None, ADD), "fs%d" % d)
+    def copy(e, a, b):
+        return V.tensor_copy(a, b) if e is V else S.activation(a, b, CP)
 
-    def gather(e, d, a, b):
-        out = T.h[:, 512 * d + 16 * a:512 * d + 16 * b]
-        win = T.pgw[:].indirect(T.off[:, 32 * d + a:32 * d + b])
-        wait(e, "fs%d" % d, 2)
-        if e is V:
-            inc(V.tensor_copy(out, win), "hv%d" % d)
+    def do(e, t):
+        k, n = t[0], int(t[1:2] or 0)
+        if k == "X":
+            chain("X", T.ps3)
+        elif k == "l":
+            ct, c = score[n]
+            for j in (1, 0):
+                i = 32 * n + 16 * j
+                inc(V.tensor_scalar(T.off[:, i:i + 16], T.base[:], T[ct][:, c + j:c + j + 1], None, ADD), "fs%d" % n)
+        elif k == "g":
+            a, b = (0, SHARE[n]) if e is V else (SHARE[n], 32)
+            wait(e, "fs%d" % n, 2)
+            inc(copy(e, T.h[:, 512 * n + 16 * a:512 * n + 16 * b], T.pgw[:].indirect(T.off[:, 32 * n + a:32 * n + b])),
+                ("hv%d" if e is V else "hs%d") % n)
+        elif k == "q":
+            if SHARE[n]:
+                wait(V, "hv%d" % n, 1)
+            wait(V, "hs%d" % n, 1)
+            inc(V.quantize_mx(T.qc[:, 128 * n:128 * n + 128], pq(n), T.h[:, 512 * n:512 * n + 512]), "qq%d" % n)
+        elif k == "L":
+            wait(V, "mp", 2 * hf)
+            for c in range(4):
+                inc(V.tensor_scalar(T.pk[:, 8 + c:32:4], T.lpk[:], 16.0 * c, None, ADD), "pl1")
+        elif k == "d":
+            wait(e, "fm%d" % n, 1)
+            inc(copy(e, T.fo[:, ALL * n:ALL * n + ALL], T["ps%d" % wbank[n]][:]), "fk%d" % n)
+        elif k == "p":
+            c = PW * (N * (n % 2) + whole[n // 2])
+            wait(e, *(("pl0", 2) if n < 2 else ("pl1", 4)))
+            wait(e, "fk%d" % n, 1)
+            inc(copy(e, T.ysb[:, c:c + PW], T.fo[:, ALL * n:ALL * n + ALL].indirect(T.pk[:, 4 * n:4 * n + 4])),
+                "y%d%d" % (n % 2, whole[n // 2]))
         else:
-            inc(S.activation(out, win, CP), "hs%d" % d)
+            j = int(t[2])
+            c = PW * (N * j + chosen[n])
+            wait(e, "m%d%d" % (j, n), 1)
+            inc(copy(e, T.ysb[:, c:c + PW], T["ps%d" % BANKS["c%d" % n][j]][:, PW * j:PW * j + PW]), "y%d%d" % (j, chosen[n]))
 
-    def quant(d):
-        for n in ("hv%d" % d, "hs%d" % d):
-            if n in total:
-                wait(V, n, 1)
-        inc(V.quantize_mx(T.qc[:, 128 * d:128 * d + 128], pq(d), T.h[:, 512 * d:512 * d + 512]), "qq%d" % d)
-
-    pe, ot = [same[(s - 1 - k) % n4] for k in range(n4 - 1)], [other[(s - k) % n4] for k in range(n4)]
-    whole, wbank = [r, ot[0], ot[1]], [5, 6, 3, 4, 5, 6]
-    order = [pe[0], pe[1], ot[2], pe[2], ot[3]]
-    banks = [(7, 0), (1, 2), (7, 0), (3, 4), (5, 6)]
-    stored = []
-
-    def drain(e, i):
-        wait(e, "fm%d" % i, 1)
-        a, b = T.fo[:, ALL * i:ALL * i + ALL], T["ps%d" % wbank[i]][:]
-        inc(V.tensor_copy(a, b) if e is V else S.activation(a, b, CP), "fk%d" % i)
-
-    def pick_lists(o, t, c):
-        for j in range(2):
-            i = 8 * o + 4 * j
-            inc(V.tensor_scalar(T.pk[:, i:i + 4], T.base4[:], t[:, c + j:c + j + 1], 0.25, ADD, MUL), "pl%d" % o)
-
-    def pick(o):
-        for j, e in enumerate((V, S)):
-            i, c = 2 * o + j, PW * (N * j + whole[o])
-            wait(e, "pl%d" % o, 2)
-            wait(e, "fk%d" % i, 1)
-            a, b = T.ysb[:, c:c + PW], T.fo[:, ALL * i:ALL * i + ALL].indirect(T.pk[:, 4 * i:4 * i + 4])
-            inc(S.activation(a, b, CP) if j else V.tensor_copy(a, b), "%s%d" % (("yv", "ys")[j], whole[o]))
-        store(whole[o])
-
-    def out(n):
-        q = order[n]
-        pa, pb = (T["ps%d" % k] for k in banks[n])
-        wait(S, "mb%d" % n, 1)
-        inc(S.activation(T.ysb[:, PW * (N + q):PW * (N + q + 1)], pb[:, PW:2 * PW], CP), "ys%d" % q)
-        wait(V, "ma%d" % n, 1)
-        inc(V.tensor_copy(T.ysb[:, PW * q:PW * (q + 1)], pa[:, 0:PW]), "yv%d" % q)
-        store(q)
-
-    def store(q):
-        stored.append(q)
-        mate = q + 1 - 2 * (q % 2)
-        if mate in stored:
-            lo = PW * min(q, mate)
-            for e, nm, a in ((S if len(stored) == N else g.sync, "ys", PW * N + lo), (g.sync, "yv", lo)):
-                for m in (mate, q):
-                    wait(e, "%s%d" % (nm, m), 1)
-                inc(e.dma_start(T.y[:, a:a + 2 * PW], T.ysb[:, a:a + 2 * PW]), "st", 16)
-
-    def choices():
-        wait(V, "cC", 1)
-        inc(V.tensor_tensor(T.ic[0:2, 1:64], T.pc[0:2, 1:64], T.pc[0:2, 0:63], GT), "cC")
-        wait(V, "cC", 2)
-        inc(V.tensor_tensor(T.jc[0:2, :], T.ic[0:2, :], T.wt[0:2, :], MUL), "cC")
-        wait(V, "cC", 3)
-        inc(V.tensor_tensor_scan(T.kc[0:2, :], T.rb[0:2, :], T.jc[0:2, :], 0.0, MIN, MAX), "cC")
-        wait(V, "cC", 4)
-        if r > 0:
-            inc(V.tensor_copy(T.chs[0:2, 0:r], T.kc[0:2, 7:8 * r:8]), "sch")
-        if r < N - 1:
-            inc(V.tensor_copy(T.chs[0:2, r + 1:N], T.kc[0:2, 8 * r + 7:56:8]), "sch")
-        inc(V.tensor_copy(T.chs[0:2, r:r + 1], T.kc[0:2, 63:64]), "sch")
-        wait(g.sync, "sch", total["sch"])
-        inc(g.sync.dma_start(T.ch[:], T.chs[0:2, :]), "st", 16)
-
-    drain(S, 0)
-    drain(S, 1)
-    chain("D", T.ps0)
-    lists(0)
-    wait(S, "ldp", 16 * PG)
-    gather(S, 0, 0, 32)
-    chain("X", T.ps1, [lambda: lists(1), lambda: lists(2), lambda: pick_lists(0, T.ctD, 6)])
-    lists(3)
-    lists(4)
-    quant(0)
-    for d in (3, 4, 1, 2):
-        gather(S, d, 14, 32)
-        gather(V, d, 0, 14)
-        quant(d)
-
-    drain(S, 3)
-    drain(S, 2)
-    wait(V, "ca", 4 * hf)
-    for o in (1, 2):
-        pick_lists(o, T.lch, 2 * o - 2)
-    pick(0)
-    pick(1)
-    drain(S, 5)
-    drain(V, 4)
-    wait(V, "tC", 1)
-    inc(V.tensor_tensor_scan(T.pc[0:2, :], T.rb[0:2, :], T.ps2[0:2, 0:64], 0.0, MIN, MAX), "cC")
-    pick(2)
-    for n in range(len(order)):
-        out(n)
-        if n == 0:
-            choices()
-
-    def product(bank, j, c, p, lo, w, n):
-        inc(TE.matmul_mx(T["ps%d" % bank][:, 0:w], T.wc[:, 128 * j:128 * j + 128], T.qp[:, 128 * j:128 * j + 128],
-                         c[:, lo:lo + w], p[:, lo:lo + w], True, True), n)
-    own = (T.smc[:, 64:192], T.smp[:, 64:192])
-    wait(TE, "fq", 1)
-    wait(TE, "wq", 1)
+    chain("O", T.ps3)
     for j in range(2):
-        product(wbank[j], j, T.fc, T.fp, 0, ALL, "fm%d" % j)
+        inc(V.tensor_scalar(T.pk[:, 4 * j:4 * j + 4], T.base4[:], T.ctO[:, j:j + 1], 0.25, ADD, MUL), "pl0")
+    chain("D", T.ps2)
+    for t in VECTOR.split():
+        do(V, t)
+    do(S, "d0")
+    do(S, "d1")
+    for i in range(3):
+        wait(S, "ldp%d" % i, 16 * len(part[i]))
+    for t in SCALAR.split():
+        do(S, t)
+
+    for pair in STORES:
+        qs = [r if w == "r" else (ot if w[0] == "w" else chosen)[int(w[1])] for w in pair.split()]
+        for j in (1, 0):
+            e = S if j and pair == STORES[-1] else g.sync
+            a = PW * (N * j + min(qs))
+            for q in qs:
+                wait(e, "y%d%d" % (j, q), 1)
+            inc(e.dma_start(T.y[:, a:a + 2 * PW], T.ysb[:, a:a + 2 * PW]), "st", 16)
+    wait(g.sync, "mc", 2 * hf)
+    for j in range(2):
+        inc(g.sync.dma_start(T.ch[j:j + 1, :], T.lch[0:N, j:j + 1]), "st", 16)
+
+    frees = {2: ("cD", 5), 3: ("cX", 5)}
+
+    def scores(bank, a, n):
+        inc(TE.matmul_mx(T["ps%d" % bank][:, 0:128], T.fc[:, 0:128], T.grp[:, SP:FP], T.grc[:, a:a + 128], T.grp[:, a:a + 128],
+                         True, True), n)
+
+    def product(bank, j, c, p, w, n, done):
+        if bank in frees:
+            wait(TE, *frees[bank])
+        frees[bank] = (done, 1)
+        inc(TE.matmul_mx(T["ps%d" % bank][:, 0:w], T.wc[:, 128 * j:128 * j + 128], T.qp[:, 128 * j:128 * j + 128], c, p, True, True), n)
     wait(TE, "vg", 1)
     wait(TE, "vs", 1)
-    wait(TE, "gd", 2 * hf * (n4 - 1))
-    inc(TE.matmul_mx(T.ps0[:, 0:128], own[0], own[1], T.grc[:, 10:138], T.grp[:, 10:138], True, True), "tD")
-    wait(TE, "gx", 4 * hf * n4)
-    inc(TE.matmul_mx(T.ps1[:, 0:128], own[0], own[1], T.grc[:, 2:130], T.grp[:, 2:130], True, True), "tX")
-    for k in range(2):
-        wait(TE, "fa%d" % k, 3 * hf * len(rel))
-        for j in range(2):
-            if k:
-                wait(TE, "fk%d" % j, 1)
-            product(wbank[2 + 2 * k + j], j, T.lfc, T.lfp, ALL * k, ALL, "fm%d" % (2 + 2 * k + j))
-    wait(TE, "sa", 4 * hf * (N - 1))
-    inc(TE.matmul_mx(T.ps2[:, 0:128], T.grc[:, 16:144], T.grp[:, 16:144], T.smc[:, 8:136], T.smp[:, 8:136], True, True), "tC")
-    freed = [[("cD", 5)], [("cX", 5), ("cC", 1)], [("yv%d" % order[0], 1), ("ys%d" % order[0], 1)],
-             [("fk2", 1), ("fk3", 1)], [("fk4", 1), ("fk5", 1)]]
-    for n, q in enumerate(order):
-        wait(TE, "pg%d" % q, 4 * hf)
-        for w in freed[n]:
-            wait(TE, *w)
+    scores(3, 16, "tO")
+    for i in range(3):
+        wait(TE, "fq%d" % i, 1)
+    wait(TE, "wq", 1)
+    for j in range(2):
+        product(wbank[j], j, T.fc[:, 128:128 + ALL], T.grp[:, FP:XP], ALL, "fm%d" % j, "fk%d" % j)
+    wait(TE, "gd", 4 * hf)
+    scores(2, 12, "tD")
+    wait(TE, "gx", 8 * hf)
+    wait(TE, "cO", 5)
+    scores(3, 8, "tX")
+    for t in TENSOR.split():
+        n = int(t[1])
+        wait(TE, *(("fa%d" % n, 8 * hf) if t[0] == "w" else ("pg%d" % chosen[n], 4 * hf)))
         for j in (1, 0):
-            product(banks[n][j], j, T.lc, T.lp, 128 * q, 128, "%s%d" % (("ma", "mb")[j], n))
-    finish()
+            if t[0] == "w":
+                i, a = 2 + 2 * n + j, ALL * n
+                product(wbank[i], j, T.lfc[:, a:a + ALL], T.lfp[:, a:a + ALL], ALL, "fm%d" % i, "fk%d" % i)
+            else:
+                a = 128 * chosen[n]
+                product(BANKS[t][j], j, T.lc[:, a:a + 128], T.lp[:, a:a + 128], 128, "m%d%d" % (j, n), "y%d%d" % (j, chosen[n]))
 
 
-def relay_part(g, T, topo, core, cores, q, s, other, i, wait, fused, send, cod, sslot):
+def relay_part(g, T, topo, core, q, calls):
+    wait, inc, fused, send = calls
+    cores = T.cores
+    same, other = classes(topo, cores, q)
+    rel, carry = helpers(topo, cores, q)
     n4 = len(other)
-    a, b = i % 2, i // 2
-    asker = [cores[other[(s + k) % n4]] for k in range(n4)]
-    es = topo.engines(core, asker[0])
+    s, i = same.index(q), rel.index(core)
+    asker = [other[(s + k) % n4] for k in range(n4)]
+    es = topo.engines(core, cores[asker[0]])
     hf = len(es) // 2
 
     def v(c, p, lo, hi):
-        return T[p][:, lo:hi] if b else cod(T[c], lo, hi)
+        return T[p][:, lo:hi] if i % 2 else cod(T[c], lo, hi)
     wait(g, "rg", hf)
-    k = 2 + 2 * s
-    fused([(v("rgc", "rgp", 0, 2), [(d, v("grc", "grp", k, k + 2)) for d in asker[a::2]], es, "gx")])
-    at = [ALL * k + 128 * i for k in range(2)]
-    wait(g, "rq", hf)
-    fused([(T.rfp[:], [(asker[k], T.lfp[:, at[k]:at[k] + 128])], es[hf * k:hf * k + hf], "fa%d" % k) for k in range(2)])
+    if i < 2:
+        to = [(cores[other[(s - NW) % n4]], v("grc", "grp", 8, 10)), (cores[same[(s + 1) % n4]], v("grc", "grp", 10, 12))]
+    else:
+        to = [(carry[0], v("egc", "egp", 128, 130))]
+    fused([(v("rgc", "rgp", 0, 2), to, es, "gx")])
     wait(g, "rf", hf)
-    for k in range(2):
-        send(cod(T.rfc, 0, 128), asker[k], cod(T.lfc, at[k], at[k] + 128), es, "fa%d" % k)
-    wait(g, "rs", hf)
-    to = [d for d in range(N) if d != q and (d in other) == (a == 0)]
-    fused([(v("rsc", "rsp", 0, 8), [(cores[d], v("smc", "smp", sslot(q, d), sslot(q, d) + 8)) for d in to], es, "sa")])
+    if i in (0, 3):
+        src = T.rfp[:, 4 * PC - ALL - PG:4 * PC - ALL] if i else cod(T.rfc, 0, PG)
+        fused([(src, [(helpers(topo, cores, asker[k])[1][0], v("esc", "esp", 128 + 8 * k, 136 + 8 * k)) for k in range(NW)], es, "sX")])
+    src = piece_of(T, i, None)
+    for k in HAND[i]:
+        if k == NW - 1 and i in DOOR:
+            send(src, doors(topo, cores[asker[k]])[DOOR[i]], src, es, "rq" if i == 3 else "rf")
+        else:
+            send(src, cores[asker[k]], piece_of(T, i, k), es, "fa%d" % k)
+    if i in LAST:
+        wait(g, "rp", len(es))
+        if i == LAST[0]:
+            send(cod(T.rpc, 0, 128), cores[asker[NW]], cod(T.lc, 128 * q, 128 * q + 128), es, "pg%d" % q)
+        else:
+            send(T.rpp[:, 384:512], cores[asker[NW]], T.lp[:, 128 * q:128 * q + 128], es, "pg%d" % q)
+
+
+def door_part(g, T, topo, core, r, calls):
+    wait, inc, fused, send = calls
+    rc = T.cores[r]
+    i = doors(topo, rc).index(core)
+    es = topo.engines(core, rc)
+    if i in (1, 2):
+        wait(g, "rs", len(es) // 2)
+        src, dst = (cod(T.rsc, 0, PG), cod(T.esc, 152, 160)) if i == 1 else (T.rsp[:, 24:32], T.esp[:, 152:160])
+        send(src, helpers(topo, T.cores, r)[1][0], dst, es, "sD")
+    for a in DOOR:
+        if DOOR[a] == i:
+            wait(g, "rq" if a == 3 else "rf", len(es))
+            send(piece_of(T, a, None), rc, piece_of(T, a, NW - 1), es, "fa%d" % (NW - 1))
+
+
+def carrier_part(g, T, topo, core, r, calls):
+    wait, inc, fused, send = calls
+    cores = T.cores
+    same, other = classes(topo, cores, r)
+    n4 = len(other)
+    s, b = same.index(r), helpers(topo, cores, r)[1].index(core)
+    es = topo.engines(core, cores[same[s - 1]])
+    if not b:
+        inc(g.iota(T.wt[:], [[0, 5], [1, 8]], 0, 0, allow_small_or_imprecise_dtypes=True), "it")
+        inc(g.iota(T.zz[:, 0:32], [[0, 2], [1, 16]], 0, 0, allow_small_or_imprecise_dtypes=True), "it")
+    at = 160 + 8 * s
+    wait(g, "rs", len(es) // 2)
+    src, dst = (T.rsp[:, 24:32], T.esp[:, at:at + 8]) if b else (cod(T.esc, at, at + 8), cod(T.esc, at, at + 8))
+    fused([(src, [(helpers(topo, cores, d)[1][0], dst) for d in same[s + 1:] + same[:s + b]], es, "sD")])
     if b:
-        wait(g, "rc", hf)
-        send(T.rch[:], asker[a], T.lch[:, 2 * a:2 * a + 2], es, "ca")
-    wait(g, "rp", len(es))
-    send(v("rpc", "rpp", 384 * b, 384 * b + 128), asker[2 + a], v("lc", "lp", 128 * q, 128 * q + 128), es, "pg%d" % q)
+        return
+
+    V, TE = g.vector, g.tensor
+    inc(V.memset(T.gsb[:], 0.0), "v0")
+    inc(V.memset(T.rb[:], BIG), "v0")
+    for t in ("icD", "icX", "kq"):
+        inc(V.memset(T[t][:], 0.0), "v0")
+    wait(V, "v0", 5)
+    inc(V.memset(T.rb[:, 0:40:8], -BIG), "v1")
+    for c, p, a in ((T.egc, T.egp, 0), (T.egc, T.egp, 144), (T.esc, T.esp, 0), (T.esc, T.esp, 192)):
+        inc(V.quantize_mx(c[:, a:a + 128], p[:, a:a + 128], T.gsb[:]), "v1")
+    wait(V, "it", 2)
+    inc(V.tensor_scalar(T.c16[:], T.zz[:, 0:32], 1.0 / PW, None, MUL), "v1")
+    wait(V, "v1", 6)
+    wait(g.sync, "v1", 6)
+    inc(g.sync.dma_start(cod(T.egc, 130, 144), cod(T.egc, 0, 14)), "eg", 16)
+    inc(g.sync.dma_start(T.egp[:, 130:144], T.egp[:, 0:14]), "eg", 16)
+    wait(TE, "v1", 6)
+    wait(TE, "eg", 32)
+    wait(TE, "gx", 2 * len(es))
+
+    def choose(b, ps):
+        pc, ic, jc, kc = (T[n + b] for n in ("pc", "ic", "jc", "kc"))
+        w = pc.shape[1]
+        wait(V, "t" + b, 1)
+        for k, step in enumerate([lambda: V.tensor_tensor_scan(pc[:], T.rb[:, 0:w], ps, 0.0, MIN, MAX),
+                                  lambda: V.tensor_tensor(ic[:, 1:w], pc[:, 1:w], pc[:, 0:w - 1], GT),
+                                  lambda: V.tensor_tensor(jc[:], ic[:], T.wt[:, 0:w], MUL),
+                                  lambda: V.tensor_tensor_scan(kc[:], T.rb[:, 0:w], jc[:], 0.0, MIN, MAX)]):
+            inc(step(), "c" + b)
+            wait(V, "c" + b, k + 1)
+
+    wait(TE, "sX", 2 * NW * len(es))
+    for a in range(4):
+        lo = 128 - 32 * a
+        mm = TE.matmul_mx(T.ps0[:, 0:128], T.egc[:, lo:lo + 128], T.egp[:, lo:lo + 128], T.esc[:, 24:152], T.esp[:, 24:152], a == 0, a == 3)
+    inc(mm, "tX")
+    choose("X", T.ps0[:, 104:128])
+    for k in range(NW):
+        inc(V.tensor_scalar(T.sp[:, 32 * k:32 * k + 32], T.c16[:], T.kcX[:, 8 * k + 7:8 * k + 8], float(PW), ADD, MUL), "v2")
+    wait(V, "v2", NW)
+    inc(V.transpose(T.st[:], T.sp[:]), "v3")
+    wait(V, "v3", 1)
+    for j in range(2):
+        inc(V.tensor_copy(T.mpk[:, j:2 * NW:2], T.st[:, j:32 * NW:32]), "em")
+    wait(g, "em", 2)
+    send(T.mpk[:], cores[r], T.lpk[:], es, "mp")
+
+    ot = [other[(s - k) % n4] for k in range(n4)]
+    for k in range(NW):
+        inc(V.tensor_copy(T.kq[:, ot[k]:ot[k] + 1], T.kcX[:, 8 * k + 7:8 * k + 8]), "v4")
+    wait(TE, "sD", (2 * n4 + 1) * len(es))
+    wait(TE, "rs", len(es) // 2)
+    inc(TE.matmul_mx(T.ps1[:, 0:128], T.egc[:, 128:256], T.egp[:, 128:256], T.esc[:, 152:280], T.esp[:, 152:280], True, True), "tD")
+    choose("D", T.ps1[:, 0:40])
+    inc(V.tensor_copy(T.kq[:, same[0]:N:same[1] - same[0]], T.kcD[:, 15:40:8]), "v4")
+    inc(V.tensor_copy(T.kq[:, ot[NW]:ot[NW] + 1], T.kcD[:, 7:8]), "v4")
+    wait(V, "v4", n4 + 1)
+    inc(V.transpose(T.kt[:], T.kq[:]), "vs")
+    wait(g, "vs", 1)
+    send(T.kt[:, 0:2], cores[r], T.lch[:], es, "mc")

from concourse.bass import DstId, RemoteDMATransfer
from concourse.mybir import dt, AluOpType, ActivationFunctionType

N, PG, PW = 8, 8, 64
E = 4 * PW
ALL = PG * PW
NW = 3
QCUT = [0, 192, 384, 512]
CUT = [0, 166, 340, 512]
PC = CUT[1] + PG
LO = [-PG, CUT[1], ALL - PC]
SP, FP = 144, 272
XP = FP + ALL
DOOR = {1: 1, 3: 2, 2: 2}
HAND = [[0, 1, 2], [0, 2, 1], [0, 2, 1], [2, 0, 1]]
LAST = (1, 3)
SHARE = [0, 12, 12, 14]

VECTOR = "l0 l1 X l3 q0 g3 l2 q3 g1 q1 g2 q2 d2 L d4 p2 p4 o00 d6 o10 p6 o30 o20"
SCALAR = "p0 p1 g0 g3 g1 g2 d3 d5 p3 p5 o01 d7 o11 p7 o31 o21"
TENSOR = "w0 w1 c0 w2 c1 c3 c2"
SERVED = [0, 3, 1, 2]
STORES = ["r w0", "c0 w1", "c1 w2", "c2 c3"]
BANKS = {"w0": (4, 5), "w1": (6, 7), "w2": (0, 1), "c0": (2, 3), "c1": (4, 5), "c2": (2, 3), "c3": (6, 7)}

F8, U8, F32, BF, I32, U16 = "float8_e4m3fn_x4", "uint8", "float32", "bfloat16", "int32", "uint16"
SCRATCH = {
    "gsb": ("sbuf", [128, 512], BF), "smr": ("sbuf", [128, 512], BF),
    "pgw": ("sbuf", [128, PG * E], BF), "qwb": ("sbuf", [128, 1024], BF),
    "grc": ("sbuf", [128, 144], F8),
    "grp": ("sbuf", [128, XP + 128], U8),
    "fc": ("sbuf", [128, 128 + ALL], F8),
    "wc": ("sbuf", [128, 256], F8),
    "h": ("sbuf", [128, 4 * 512], BF),
    "qc": ("sbuf", [128, 4 * 128], F8), "qp": ("sbuf", [128, 5 * 128], U8),
    "lc": ("sbuf", [128, N * 128], F8), "lp": ("sbuf", [128, N * 128], U8),
    "lfc": ("sbuf", [128, NW * ALL], F8), "lfp": ("sbuf", [128, NW * ALL], U8),
    "lpk": ("sbuf", [128, 2 * NW], U16), "lch": ("sbuf", [128, 2], F32),
    "rgc": ("sbuf", [128, 2], F8), "rgp": ("sbuf", [128, 8], U8),
    "rsc": ("sbuf", [128, 8], F8), "rsp": ("sbuf", [128, 32], U8),
    "rfc": ("sbuf", [128, PC], F8), "rfp": ("sbuf", [128, 4 * PC], U8),
    "rpc": ("sbuf", [128, 128], F8), "rpp": ("sbuf", [128, 512], U8),
    "egc": ("sbuf", [128, 272], F8), "egp": ("sbuf", [128, 272], U8),
    "esc": ("sbuf", [128, 320], F8), "esp": ("sbuf", [128, 320], U8),
    "rb": ("sbuf", [128, 40], F32), "wt": ("sbuf", [128, 40], F32), "c16": ("sbuf", [128, 32], F32),
    "sp": ("sbuf", [128, 32 * NW], F32), "st": ("sbuf", [128, 32 * NW], F32), "mpk": ("sbuf", [128, 2 * NW], U16),
    "kq": ("sbuf", [128, 32], F32), "kt": ("sbuf", [128, 32], F32),
    "zz": ("sbuf", [128, 64], F32),
    "ta": ("sbuf", [128, 16], I32), "tb": ("sbuf", [128, 16], I32), "tc": ("sbuf", [128, 16], I32),
    "base": ("sbuf", [128, 16], F32), "base4": ("sbuf", [128, 4], F32),
    "off": ("sbuf", [128, 4 * 32], U16), "pk": ("sbuf", [128, 8 * 4], U16),
    "fo": ("sbuf", [128, 8 * ALL], F32),
    "ysb": ("sbuf", [128, 1024], F32),
}
for _b in "ODX":
    for _n, _w in (("ts", 32), ("pm", 8), ("ind", 64), ("cc", 64), ("ct", 32)):
        SCRATCH[_n + _b] = ("sbuf", [128, _w], F32)
for _b, _w in (("D", 40), ("X", 24)):
    for _n in ("pc", "ic", "jc", "kc"):
        SCRATCH[_n + _b] = ("sbuf", [128, _w], F32)
for _i in range(8):
    SCRATCH["ps%d" % _i] = ("psum", [128, 512], F32)
SEMAPHORES = (["ldg", "lds", "ldw", "v0", "vg", "v1", "vs", "v2", "v3", "v4", "v5", "it", "gd", "gx", "tO", "tD", "tX", "cO", "cD",
               "cX", "wq", "rg", "rs", "rf", "rq", "rp", "eg", "sD", "sX", "em", "mp", "mc", "pl0", "pl1", "ls", "st"]
              + ["%s%d" % (n, i) for n in ("ldp", "fq", "fa") for i in range(3)]
              + ["%s%d" % (n, i) for n in ("fs", "hv", "hs", "qq", "m0", "m1") for i in range(4)]
              + ["%s%d" % (n, i) for n in ("fm", "fk", "pg", "y0", "y1") for i in range(8)])
BIG = 1e29
ADD, MAX, MIN, MUL = AluOpType.add, AluOpType.max, AluOpType.min, AluOpType.mult
LT, GT = AluOpType.is_lt, AluOpType.is_gt


def classes(topo, cores, r):
    same = [q for q in range(N) if q == r or topo.same_plane(cores[q], cores[r])]
    return same, [q for q in range(N) if q not in same]


def helpers(topo, cores, r):
    rc, far = cores[r], [cores[d] for d in classes(topo, cores, r)[1]]
    c = [x for x in topo.cores_of(rc) if x != rc]
    rel = [x for x in c if all(topo.may_write(x, d) for d in far)]
    near = [x for x in c if topo.die(x) == topo.die(rc)]
    return [x for x in rel if x not in near] + [x for x in rel if x in near], [x for x in c if x not in rel and x not in near]


def doors(topo, rc):
    c = [x for x in range(256) if topo.mates(x, rc) and topo.may_write(x, rc)]
    return [x for x in c if topo.die(x) != topo.die(rc)] + [x for x in c if topo.die(x) == topo.die(rc)]


def mask(es):
    m = 0
    for e in es:
        m |= 1 << e
    return m


def cod(t, a, b):
    return t[:, a:b].bitcast(dt.uint8)


def piece_of(T, i, k):
    if k is None:
        return cod(T.rfc, CUT[i] - LO[i], CUT[i + 1] - LO[i]) if i < 3 else T.rfp[:, 4 * PC - ALL:4 * PC]
    return cod(T.lfc, ALL * k + CUT[i], ALL * k + CUT[i + 1]) if i < 3 else T.lfp[:, ALL * k:ALL * k + ALL]


def rank_program(g, core, T, topo):
    cores = T.cores
    total, waited = {}, {}

    def wait(eng, n, v):
        eng.wait_ge(T.sem[n], v)
        waited[n] = max(waited.get(n, 0), v)

    def inc(inst, n, v=1):
        inst.then_inc(T.sem[n], v)
        total[n] = total.get(n, 0) + v

    def fused(parts):
        tr = []
        for src, dsts, es, s in parts:
            ids = []
            for d, _ in dsts:
                rid, pid = topo.addr(d, core)
                ids.append(DstId(rid=rid, pnc=pid))
            tr.append(RemoteDMATransfer(dst_ids=ids, dma_engine_mask=mask(es), remote_sem=T.sem[s],
                                        srcs=[src], dsts=[a for _, a in dsts]))
            total["ls"] = total.get("ls", 0) + len(es)
        g.remote_dma_fused(tr, local_sem=T.sem["ls"])

    def send(src, d, dst, es, s):
        rid, pid = topo.addr(d, core)
        g.remote_dma(dst, src, T.sem[s], T.sem["ls"], pid, rid, mask(es))
        total["ls"] = total.get("ls", 0) + len(es)

    calls = (wait, inc, fused, send)
    for r in range(N):
        if topo.mates(core, cores[r]) and core in doors(topo, cores[r]):
            door_part(g, T, topo, core, r, calls)
        if core in topo.cores_of(cores[r]):
            rel, carry = helpers(topo, cores, r)
            if core == cores[r]:
                rank_part(g, T, topo, r, calls)
            elif core in rel:
                relay_part(g, T, topo, core, r, calls)
            elif core in carry:
                carrier_part(g, T, topo, core, r, calls)
    for n in total:
        if waited.get(n, 0) < total[n]:
            g.wait_ge(T.sem[n], total[n])


def rank_part(g, T, topo, r, calls):
    wait, inc, fused, send = calls
    cores = T.cores
    core = cores[r]
    same, other = classes(topo, cores, r)
    rel, carry = helpers(topo, cores, r)
    n4 = len(same)
    s = same.index(r)
    dD = [same[(s + 1 + k) % n4] for k in range(n4 - 1)]
    off = topo.engines(core, cores[dD[0]])
    far = [e for e in topo.engines(core, rel[0]) if e not in off]
    hf = len(off) // 2
    quads = [far[0::2], far[1::2], off[0::2], off[1::2]]
    V, S, TE = g.vector, g.scalar, g.tensor
    CP = ActivationFunctionType.Copy

    inc(g.sync.dma_start(T.gsb[:, 0:8], T.gs[:, 0:8]), "ldg", 16)
    inc(S.dma_start(T.smr[:, 96:128], T.sm[:, 0:32]), "lds", 16)
    part = [[m for m in range(PG) if QCUT[i] <= PW * m < QCUT[i + 1]] for i in range(3)]
    for i in range(3):
        for m in part[i]:
            e = g.sync if m % 2 == 0 else S
            inc(e.dma_start(T.pgw[:, E * m:E * m + E], T.pg[128 * m:128 * m + 128, :]), "ldp%d" % i, 16)
    inc(g.sync.dma_start(T.qwb[:], T.qw[:]), "ldw", 16)

    inc(g.iota(T.ta[:], [[0, 16]], 0, 1), "it")
    inc(g.iota(T.tb[:], [[16, 16]], 0, 0), "it")
    slot = [(cores[dD[k]], 10 + 2 * k) for k in (1, 2)]
    wait(g, "vg", 1)
    fused([(cod(T.grc, 16, 18), [(a, cod(T.rgc, 0, 2)) for a in rel[0::2]], quads[0], "rg"),
           (T.grp[:, 16:24], [(a, T.rgp[:]) for a in rel[1::2]], quads[1], "rg"),
           (cod(T.grc, 16, 18), [(d, cod(T.grc, a, a + 2)) for d, a in slot], quads[2], "gd")])
    fused([(T.grp[:, 16:18], [(d, T.grp[:, a:a + 2]) for d, a in slot], quads[3], "gd")])
    wait(g, "vs", 1)
    for i in range(3):
        wait(g, "fq%d" % i, 1)
    runs = [cod(T.fc, 128 + LO[i], 128 + LO[i] + PC) for i in range(3)] + [T.grp[:, XP - 4 * PC:XP]]
    fused([(runs[i], [(rel[i], cod(T.rfc, 0, PC) if i < 3 else T.rfp[:])], quads[(0, 2, 3, 1)[i]], "rf") for i in range(4)])
    door = doors(topo, cores[other[(s + NW) % n4]])
    smc, smp = cod(T.fc, 128 - PG, 128), T.grp[:, FP - 32:FP]
    fused([(smc, [(carry[0], cod(T.esc, 160 + 8 * s, 168 + 8 * s))], quads[0], "rs"), (smp, [(carry[1], T.rsp[:])], quads[1], "rs"),
           (smc, [(door[1], cod(T.rsc, 0, PG))], quads[2], "rs"), (smp, [(door[2], T.rsp[:])], quads[3], "rs")])

    def cq(d):
        return cod(T.qc, 128 * d, 128 * d + 128)

    def pq(d):
        return T.qp[:, 256 + 128 * d:384 + 128 * d] if d < 3 else T.grp[:, XP:XP + 128]
    for d in SERVED:
        wait(g, "qq%d" % d, 1)
        if d < 3:
            send(cq(d), cores[dD[d]], cod(T.lc, 128 * r, 128 * r + 128), off, "pg%d" % r)
            fused([(pq(d), [(cores[dD[d]], T.lp[:, 128 * r:128 * r + 128])], off, "pg%d" % r)])
        else:
            fused([(cq(d), [(rel[LAST[0]], cod(T.rpc, 0, 128))], far, "rp"),
                   (T.grp[:, XP - 384:XP + 128], [(rel[LAST[1]], T.rpp[:])], off, "rp")])

    inc(V.memset(T.gsb[:, 8:512], 0.0), "v0")
    inc(V.memset(T.smr[:, 0:96], 0.0), "v5")
    for t in ("zz", "indO", "indD", "indX"):
        inc(V.memset(T[t][:], 0.0), "v2")
    wait(V, "v0", 1)
    wait(V, "ldg", 16)
    inc(V.quantize_mx(T.grc[:, 16:144], T.grp[:, 16:144], T.gsb[:]), "vg")
    wait(V, "lds", 16)
    wait(V, "v5", 1)
    inc(V.tensor_copy(T.smr[:, 128:256], T.smr[:, 0:128]), "v1")
    wait(V, "it", 2)
    inc(V.tensor_scalar(T.tc[:], T.ta[:], 15, None, AluOpType.bitwise_and), "v2")
    wait(V, "v1", 1)
    inc(V.tensor_copy(T.smr[:, 256:512], T.smr[:, 0:256]), "v1")
    wait(V, "v2", 5)
    inc(V.tensor_tensor(T.base[:], T.tc[:], T.tb[:], ADD), "v3")
    wait(V, "v1", 2)
    inc(V.quantize_mx(T.fc[:, 0:128], T.grp[:, SP:FP], T.smr[:]), "vs")
    wait(V, "v3", 1)
    inc(V.tensor_scalar(T.base4[:], T.base[:, 0:4], 4.0, None, MUL), "v4")
    for i in range(3):
        wait(V, "ldp%d" % i, 16 * len(part[i]))
        a, b = QCUT[i], QCUT[i + 1]
        inc(V.quantize_mx(T.fc[:, 128 + a:128 + b], T.grp[:, FP + a:FP + b], T.pgw[:, 4 * a:4 * b]), "fq%d" % i)
    wait(V, "ldw", 16)
    inc(V.quantize_mx(T.wc[:], T.qp[:, 0:256], T.qwb[:]), "wq")
    wait(V, "v4", 1)

    pe, ot = [same[(s - 1 - k) % n4] for k in range(n4 - 1)], [other[(s - k) % n4] for k in range(n4)]
    whole, chosen = [r] + ot[:NW], pe + ot[NW:]
    wbank = [0, 1] + [b for k in range(NW) for b in BANKS["w%d" % k]]
    score = [("ctD", 2), ("ctD", 0), ("ctX", 2), ("ctX", 0)]

    def chain(b, ps):
        c = "c" + b
        ts, pm, ind, cc, ct = (T[n + b] for n in ("ts", "pm", "ind", "cc", "ct"))
        steps = [lambda: V.transpose(ts[:], ps[:, 0:32]),
                 lambda: V.tensor_tensor_scan(pm[:], T.zz[:, 0:8], ts[:, 24:32], -BIG, ADD, MAX),
                 lambda: V.tensor_scalar(ind[:, 24:32], pm[:], pm[:, 7:8], float(E), LT, MUL),
                 lambda: V.tensor_tensor_scan(cc[:, 24:64], ind[:, 24:64], T.zz[:, 0:40], 0.0, ADD, ADD),
                 lambda: V.transpose(ct[:], cc[:, 32:64])]
        wait(V, "t" + b, 1)
        for k, step in enumerate(steps):
            inc(step(), c)
            wait(V, c, k + 1)

    def copy(e, a, b):
        return V.tensor_copy(a, b) if e is V else S.activation(a, b, CP)

    def do(e, t):
        k, n = t[0], int(t[1:2] or 0)
        if k == "X":
            chain("X", T.ps3)
        elif k == "l":
            ct, c = score[n]
            for j in (1, 0):
                i = 32 * n + 16 * j
                inc(V.tensor_scalar(T.off[:, i:i + 16], T.base[:], T[ct][:, c + j:c + j + 1], None, ADD), "fs%d" % n)
        elif k == "g":
            a, b = (0, SHARE[n]) if e is V else (SHARE[n], 32)
            wait(e, "fs%d" % n, 2)
            inc(copy(e, T.h[:, 512 * n + 16 * a:512 * n + 16 * b], T.pgw[:].indirect(T.off[:, 32 * n + a:32 * n + b])),
                ("hv%d" if e is V else "hs%d") % n)
        elif k == "q":
            if SHARE[n]:
                wait(V, "hv%d" % n, 1)
            wait(V, "hs%d" % n, 1)
            inc(V.quantize_mx(T.qc[:, 128 * n:128 * n + 128], pq(n), T.h[:, 512 * n:512 * n + 512]), "qq%d" % n)
        elif k == "L":
            wait(V, "mp", 2 * hf)
            for c in range(4):
                inc(V.tensor_scalar(T.pk[:, 8 + c:32:4], T.lpk[:], 16.0 * c, None, ADD), "pl1")
        elif k == "d":
            wait(e, "fm%d" % n, 1)
            inc(copy(e, T.fo[:, ALL * n:ALL * n + ALL], T["ps%d" % wbank[n]][:]), "fk%d" % n)
        elif k == "p":
            c = PW * (N * (n % 2) + whole[n // 2])
            wait(e, *(("pl0", 2) if n < 2 else ("pl1", 4)))
            wait(e, "fk%d" % n, 1)
            inc(copy(e, T.ysb[:, c:c + PW], T.fo[:, ALL * n:ALL * n + ALL].indirect(T.pk[:, 4 * n:4 * n + 4])),
                "y%d%d" % (n % 2, whole[n // 2]))
        else:
            j = int(t[2])
            c = PW * (N * j + chosen[n])
            wait(e, "m%d%d" % (j, n), 1)
            inc(copy(e, T.ysb[:, c:c + PW], T["ps%d" % BANKS["c%d" % n][j]][:, PW * j:PW * j + PW]), "y%d%d" % (j, chosen[n]))

    chain("O", T.ps3)
    for j in range(2):
        inc(V.tensor_scalar(T.pk[:, 4 * j:4 * j + 4], T.base4[:], T.ctO[:, j:j + 1], 0.25, ADD, MUL), "pl0")
    chain("D", T.ps2)
    for t in VECTOR.split():
        do(V, t)
    do(S, "d0")
    do(S, "d1")
    for i in range(3):
        wait(S, "ldp%d" % i, 16 * len(part[i]))
    for t in SCALAR.split():
        do(S, t)

    for pair in STORES:
        qs = [r if w == "r" else (ot if w[0] == "w" else chosen)[int(w[1])] for w in pair.split()]
        for j in (1, 0):
            e = S if j and pair == STORES[-1] else g.sync
            a = PW * (N * j + min(qs))
            for q in qs:
                wait(e, "y%d%d" % (j, q), 1)
            inc(e.dma_start(T.y[:, a:a + 2 * PW], T.ysb[:, a:a + 2 * PW]), "st", 16)
    wait(g.sync, "mc", 2 * hf)
    for j in range(2):
        inc(g.sync.dma_start(T.ch[j:j + 1, :], T.lch[0:N, j:j + 1]), "st", 16)

    frees = {2: ("cD", 5), 3: ("cX", 5)}

    def scores(bank, a, n):
        inc(TE.matmul_mx(T["ps%d" % bank][:, 0:128], T.fc[:, 0:128], T.grp[:, SP:FP], T.grc[:, a:a + 128], T.grp[:, a:a + 128],
                         True, True), n)

    def product(bank, j, c, p, w, n, done):
        if bank in frees:
            wait(TE, *frees[bank])
        frees[bank] = (done, 1)
        inc(TE.matmul_mx(T["ps%d" % bank][:, 0:w], T.wc[:, 128 * j:128 * j + 128], T.qp[:, 128 * j:128 * j + 128], c, p, True, True), n)
    wait(TE, "vg", 1)
    wait(TE, "vs", 1)
    scores(3, 16, "tO")
    for i in range(3):
        wait(TE, "fq%d" % i, 1)
    wait(TE, "wq", 1)
    for j in range(2):
        product(wbank[j], j, T.fc[:, 128:128 + ALL], T.grp[:, FP:XP], ALL, "fm%d" % j, "fk%d" % j)
    wait(TE, "gd", 4 * hf)
    scores(2, 12, "tD")
    wait(TE, "gx", 8 * hf)
    wait(TE, "cO", 5)
    scores(3, 8, "tX")
    for t in TENSOR.split():
        n = int(t[1])
        wait(TE, *(("fa%d" % n, 8 * hf) if t[0] == "w" else ("pg%d" % chosen[n], 4 * hf)))
        for j in (1, 0):
            if t[0] == "w":
                i, a = 2 + 2 * n + j, ALL * n
                product(wbank[i], j, T.lfc[:, a:a + ALL], T.lfp[:, a:a + ALL], ALL, "fm%d" % i, "fk%d" % i)
            else:
                a = 128 * chosen[n]
                product(BANKS[t][j], j, T.lc[:, a:a + 128], T.lp[:, a:a + 128], 128, "m%d%d" % (j, n), "y%d%d" % (j, chosen[n]))


def relay_part(g, T, topo, core, q, calls):
    wait, inc, fused, send = calls
    cores = T.cores
    same, other = classes(topo, cores, q)
    rel, carry = helpers(topo, cores, q)
    n4 = len(other)
    s, i = same.index(q), rel.index(core)
    asker = [other[(s + k) % n4] for k in range(n4)]
    es = topo.engines(core, cores[asker[0]])
    hf = len(es) // 2

    def v(c, p, lo, hi):
        return T[p][:, lo:hi] if i % 2 else cod(T[c], lo, hi)
    wait(g, "rg", hf)
    if i < 2:
        to = [(cores[other[(s - NW) % n4]], v("grc", "grp", 8, 10)), (cores[same[(s + 1) % n4]], v("grc", "grp", 10, 12))]
    else:
        to = [(carry[0], v("egc", "egp", 128, 130))]
    fused([(v("rgc", "rgp", 0, 2), to, es, "gx")])
    wait(g, "rf", hf)
    if i in (0, 3):
        src = T.rfp[:, 4 * PC - ALL - PG:4 * PC - ALL] if i else cod(T.rfc, 0, PG)
        fused([(src, [(helpers(topo, cores, asker[k])[1][0], v("esc", "esp", 128 + 8 * k, 136 + 8 * k)) for k in range(NW)], es, "sX")])
    src = piece_of(T, i, None)
    for k in HAND[i]:
        if k == NW - 1 and i in DOOR:
            send(src, doors(topo, cores[asker[k]])[DOOR[i]], src, es, "rq" if i == 3 else "rf")
        else:
            send(src, cores[asker[k]], piece_of(T, i, k), es, "fa%d" % k)
    if i in LAST:
        wait(g, "rp", len(es))
        if i == LAST[0]:
            send(cod(T.rpc, 0, 128), cores[asker[NW]], cod(T.lc, 128 * q, 128 * q + 128), es, "pg%d" % q)
        else:
            send(T.rpp[:, 384:512], cores[asker[NW]], T.lp[:, 128 * q:128 * q + 128], es, "pg%d" % q)


def door_part(g, T, topo, core, r, calls):
    wait, inc, fused, send = calls
    rc = T.cores[r]
    i = doors(topo, rc).index(core)
    es = topo.engines(core, rc)
    if i in (1, 2):
        wait(g, "rs", len(es) // 2)
        src, dst = (cod(T.rsc, 0, PG), cod(T.esc, 152, 160)) if i == 1 else (T.rsp[:, 24:32], T.esp[:, 152:160])
        send(src, helpers(topo, T.cores, r)[1][0], dst, es, "sD")
    for a in DOOR:
        if DOOR[a] == i:
            wait(g, "rq" if a == 3 else "rf", len(es))
            send(piece_of(T, a, None), rc, piece_of(T, a, NW - 1), es, "fa%d" % (NW - 1))


def carrier_part(g, T, topo, core, r, calls):
    wait, inc, fused, send = calls
    cores = T.cores
    same, other = classes(topo, cores, r)
    n4 = len(other)
    s, b = same.index(r), helpers(topo, cores, r)[1].index(core)
    es = topo.engines(core, cores[same[s - 1]])
    if not b:
        inc(g.iota(T.wt[:], [[0, 5], [1, 8]], 0, 0, allow_small_or_imprecise_dtypes=True), "it")
        inc(g.iota(T.zz[:, 0:32], [[0, 2], [1, 16]], 0, 0, allow_small_or_imprecise_dtypes=True), "it")
    at = 160 + 8 * s
    wait(g, "rs", len(es) // 2)
    src, dst = (T.rsp[:, 24:32], T.esp[:, at:at + 8]) if b else (cod(T.esc, at, at + 8), cod(T.esc, at, at + 8))
    fused([(src, [(helpers(topo, cores, d)[1][0], dst) for d in same[s + 1:] + same[:s + b]], es, "sD")])
    if b:
        return

    V, TE = g.vector, g.tensor
    inc(V.memset(T.gsb[:], 0.0), "v0")
    inc(V.memset(T.rb[:], BIG), "v0")
    for t in ("icD", "icX", "kq"):
        inc(V.memset(T[t][:], 0.0), "v0")
    wait(V, "v0", 5)
    inc(V.memset(T.rb[:, 0:40:8], -BIG), "v1")
    for c, p, a in ((T.egc, T.egp, 0), (T.egc, T.egp, 144), (T.esc, T.esp, 0), (T.esc, T.esp, 192)):
        inc(V.quantize_mx(c[:, a:a + 128], p[:, a:a + 128], T.gsb[:]), "v1")
    wait(V, "it", 2)
    inc(V.tensor_scalar(T.c16[:], T.zz[:, 0:32], 1.0 / PW, None, MUL), "v1")
    wait(V, "v1", 6)
    wait(g.sync, "v1", 6)
    inc(g.sync.dma_start(cod(T.egc, 130, 144), cod(T.egc, 0, 14)), "eg", 16)
    inc(g.sync.dma_start(T.egp[:, 130:144], T.egp[:, 0:14]), "eg", 16)
    wait(TE, "v1", 6)
    wait(TE, "eg", 32)
    wait(TE, "gx", 2 * len(es))

    def choose(b, ps):
        pc, ic, jc, kc = (T[n + b] for n in ("pc", "ic", "jc", "kc"))
        w = pc.shape[1]
        wait(V, "t" + b, 1)
        for k, step in enumerate([lambda: V.tensor_tensor_scan(pc[:], T.rb[:, 0:w], ps, 0.0, MIN, MAX),
                                  lambda: V.tensor_tensor(ic[:, 1:w], pc[:, 1:w], pc[:, 0:w - 1], GT),
                                  lambda: V.tensor_tensor(jc[:], ic[:], T.wt[:, 0:w], MUL),
                                  lambda: V.tensor_tensor_scan(kc[:], T.rb[:, 0:w], jc[:], 0.0, MIN, MAX)]):
            inc(step(), "c" + b)
            wait(V, "c" + b, k + 1)

    wait(TE, "sX", 2 * NW * len(es))
    for a in range(4):
        lo = 128 - 32 * a
        mm = TE.matmul_mx(T.ps0[:, 0:128], T.egc[:, lo:lo + 128], T.egp[:, lo:lo + 128], T.esc[:, 24:152], T.esp[:, 24:152], a == 0, a == 3)
    inc(mm, "tX")
    choose("X", T.ps0[:, 104:128])
    for k in range(NW):
        inc(V.tensor_scalar(T.sp[:, 32 * k:32 * k + 32], T.c16[:], T.kcX[:, 8 * k + 7:8 * k + 8], float(PW), ADD, MUL), "v2")
    wait(V, "v2", NW)
    inc(V.transpose(T.st[:], T.sp[:]), "v3")
    wait(V, "v3", 1)
    for j in range(2):
        inc(V.tensor_copy(T.mpk[:, j:2 * NW:2], T.st[:, j:32 * NW:32]), "em")
    wait(g, "em", 2)
    send(T.mpk[:], cores[r], T.lpk[:], es, "mp")

    ot = [other[(s - k) % n4] for k in range(n4)]
    for k in range(NW):
        inc(V.tensor_copy(T.kq[:, ot[k]:ot[k] + 1], T.kcX[:, 8 * k + 7:8 * k + 8]), "v4")
    wait(TE, "sD", (2 * n4 + 1) * len(es))
    wait(TE, "rs", len(es) // 2)
    inc(TE.matmul_mx(T.ps1[:, 0:128], T.egc[:, 128:256], T.egp[:, 128:256], T.esc[:, 152:280], T.esp[:, 152:280], True, True), "tD")
    choose("D", T.ps1[:, 0:40])
    inc(V.tensor_copy(T.kq[:, same[0]:N:same[1] - same[0]], T.kcD[:, 15:40:8]), "v4")
    inc(V.tensor_copy(T.kq[:, ot[NW]:ot[NW] + 1], T.kcD[:, 7:8]), "v4")
    wait(V, "v4", n4 + 1)
    inc(V.transpose(T.kt[:], T.kq[:]), "vs")
    wait(g, "vs", 1)
    send(T.kt[:, 0:2], cores[r], T.lch[:], es, "mc")
